import numpy as np
import ml_dtypes


def mxq(x, axis, fmt="e4m3"):
    dtype, down = {"e4m3": (ml_dtypes.float8_e4m3fn, 7), "e5m2": (ml_dtypes.float8_e5m2, 14)}[fmt]
    v = np.moveaxis(np.asarray(x, np.float32).astype(ml_dtypes.bfloat16).astype(np.float64), axis, -1)
    blocks = v.reshape(v.shape[:-1] + (-1, 32))
    amax = np.abs(blocks).max(-1, keepdims=True)
    byte = np.maximum(np.where(amax > 0, np.frexp(amax)[1] - 1 + 127, 0) - down, 1)
    scale = np.exp2(byte - 127.0)
    codes = (blocks / scale).astype(np.float32).astype(dtype).astype(np.float64)
    return np.moveaxis((codes * scale).reshape(v.shape), -1, axis)


WIDE = False


def mx_kscale(k):
    if not WIDE:
        return np.ones(k)
    levels = np.array([10, -10, 5, -5, 0])
    if k % 512:
        return np.exp2(np.random.permutation(np.resize(levels, k // 32))).repeat(32)
    a = np.empty((k // 512, 16))
    for p in range(k // 512):
        a[p, :8] = np.random.permutation(np.resize(levels, 8))
        for g in range(8):
            far = levels[np.abs(levels - a[p, g]) >= 10]
            a[p, g + 8] = far[np.random.randint(len(far))]
    return np.exp2(a.ravel()).repeat(32)


def f64(x):
    return np.asarray(x).astype(np.float64)


def striped(idx):
    return np.tile(idx.reshape(-1, 16).T, (8, 1)).astype(np.uint16)


def unstriped(offs):
    return offs[:16].T.reshape(-1).astype(np.int64)


def striped8(idx):
    return np.concatenate([x.reshape(-1, 16).T for x in idx]).astype(np.uint16)


def runs(offs, k):
    lists = np.stack([offs[16 * r : 16 * r + 16].T.reshape(-1) for r in range(8)]).astype(np.int64)
    return lists[np.arange(k) % 512 // 64]


def pack_weight(w):
    k, n = w.shape
    w = f64(np.asarray(w, np.float32).astype(ml_dtypes.bfloat16)).reshape(k // 32, 32, n)
    amax = np.abs(w).max(1)
    byte = np.clip(np.where(amax > 0, np.frexp(amax)[1] - 1 + 127 - 7, 1), 1, 254)
    scaled = (w * np.exp2(127.0 - byte)[:, None, :]).reshape(k, n).astype(np.float32)
    words = np.ascontiguousarray(scaled.reshape(k // 512, 128, 4, n).transpose(0, 1, 3, 2)).astype(ml_dtypes.float8_e4m3fn).view(np.uint8)
    return words, np.ascontiguousarray(byte.astype(np.uint8).reshape(k // 512, 16, n))


def unpack_weight(words, scales):
    g, p, n, _ = words.shape
    vals = np.ascontiguousarray(words).view(ml_dtypes.float8_e4m3fn).astype(np.float64) * np.repeat(np.exp2(scales.astype(np.float64) - 127.0), 8, axis=1)[..., None]
    return vals.transpose(0, 1, 3, 2).reshape(g * 512, n)


K, T, S, V, N, G, H = 512, 2048, 1024, 512, 512, 2048, 512


def setup_inputs():
    n = np.random.standard_normal
    s = mx_kscale(K)[:, None]
    u = mx_kscale(H)
    packed_xT = pack_weight(n((K, T)) * s)
    packed_dT = pack_weight(n((K, G)) / s)
    return {
        "x_words": packed_xT[0],
        "x_scales": packed_xT[1],
        "d_words": packed_dT[0],
        "d_scales": packed_dT[1],
        "gn": (np.random.uniform(0.5, 1.5, (H, 1)) * u[:, None]).astype(np.float32),
        "w1": (n((H, N)) / np.sqrt(H) / u[:, None]).astype(np.float32),
        "offs": striped(np.random.permutation(T)[:S]),
        "kidx": striped8(np.random.randint(0, G, (8, H))),
    }


def reference(x_words, x_scales, d_words, d_scales, gn, w1, offs, kidx):
    d_kidx = unpack_weight(d_words, d_scales)[np.arange(K)[:, None], runs(kidx, K)]
    xq = unpack_weight(x_words, x_scales)[:, unstriped(offs)]
    s = 0.0625 * (d_kidx.T @ xq)
    mx = s.reshape(H, V, 2).max(axis=2)
    z = f64(gn) * mx
    return mxq(f64(w1), 0, "e4m3").T @ mxq(z, 0, "e4m3")

@@ -1,0 +1,164 @@
+from contextlib import ExitStack
+
+import concourse.mybir as mybir
+
+K, T, S, V, N, G, H = 512, 2048, 1024, 512, 512, 2048, 512
+FLOPS = 2 * K * H * S + 2 * H * N * V
+
+F32 = mybir.dt.float32
+BF16 = mybir.dt.bfloat16
+I32 = mybir.dt.int32
+U32 = mybir.dt.uint32
+U16 = mybir.dt.uint16
+U8 = mybir.dt.uint8
+FP8X4 = mybir.dt.float8_e4m3fn_x4
+ACT = mybir.ActivationFunctionType
+ALU = mybir.AluOpType
+
+P = 128
+PACK = 4
+CHUNKS = 4
+TOK = S // CHUNKS
+PAS = V // CHUNKS
+GROUPS = ((0,), (1,), (2,), (3,))
+
+
+def tile_picked_scorepool_none_p_kernel(tc, x_words, x_scales, d_words, d_scales, gn, w1, offs, kidx, out):
+    nc = tc.nc
+    with ExitStack() as ctx:
+        keep = ctx.enter_context(tc.tile_pool(name="keep", bufs=1))
+        psum = ctx.enter_context(tc.psum_pool(name="psum", bufs=8))
+
+        kidx_t = keep.tile([P, H // 16], U16, name="kidx_t")
+        offs_t = keep.tile([P, S // 16], U16, name="offs_t")
+        d_word_win = keep.tile([P, G], U32, name="d_word_win", align_bytes=64)
+        x_word_win = keep.tile([P, T], U32, name="x_word_win", align_bytes=64)
+        d_byte_win = keep.tile([P, G], U8, name="d_byte_win", align_bytes=64)
+        x_byte_win = keep.tile([P, T], U8, name="x_byte_win", align_bytes=64)
+        w_raw = [keep.tile([P, 2, N], F32, name="w_raw%d" % h) for h in range(2)]
+        gn_t = keep.tile([P, PACK], F32, name="gn_t")
+
+        nc.vector.memset(d_byte_win[:].bitcast(I32), 0)
+        nc.vector.memset(x_byte_win[:].bitcast(I32), 0)
+
+        w_view = w1.rearrange("(p t) m -> p t m", t=PACK)
+        nc.sync.dma_start(kidx_t[:], kidx)
+        nc.sync.dma_start(offs_t[:], offs)
+        nc.sync.dma_start(out=gn_t[:], in_=gn.rearrange("(p t) o -> p (t o)", t=PACK))
+        nc.sync.dma_start(out=d_byte_win[0:P:8, :].bitcast(I32), in_=d_scales[0].bitcast(I32))
+        for h in range(2):
+            nc.sync.dma_start(out=w_raw[h][:], in_=w_view[:, 2 * h : 2 * h + 2, :])
+        for r in range(4):
+            nc.sync.dma_start(out=x_byte_win[r:P:32, :].bitcast(I32), in_=x_scales[0, r:16:4, :].bitcast(I32))
+        nc.sync.dma_start(out=d_word_win[:].bitcast(I32), in_=d_words[0].rearrange("p n t -> p (n t)").bitcast(I32))
+        nc.sync.dma_start(out=x_word_win[:].bitcast(I32), in_=x_words[0].rearrange("p n t -> p (n t)").bitcast(I32))
+
+        g_size = keep.tile([P, PACK], F32, name="g_size")
+        g_sign = keep.tile([P, PACK], F32, name="g_sign")
+        nc.scalar.activation(g_sign[:], gn_t[:], ACT.Sign)
+        nc.scalar.activation(g_size[:], gn_t[:], ACT.Abs, scale=0.0625)
+
+        d_bytes = keep.tile([P, H], U8, name="d_bytes", align_bytes=64)
+        nc.vector.tensor_copy(d_bytes[:], d_byte_win[:].indirect(kidx_t[:]))
+        key_scales = keep.tile([P, H], U8, name="key_scales", align_bytes=64)
+        nc.vector.tensor_copy(key_scales[:].rearrange("p (t m) -> p t m", t=PACK), d_bytes[:].rearrange("p (m t) -> p t m", t=PACK))
+        for r in range(1, 4):
+            nc.sync.dma_start(out=key_scales[r:P:32, :].bitcast(I32), in_=key_scales[8 * r : P : 32, :].bitcast(I32))
+
+        tok_scales = keep.tile([P, S], U8, name="tok_scales", align_bytes=64)
+        nc.vector.tensor_copy(tok_scales[:], x_byte_win[:].indirect(offs_t[:]))
+
+        w_signed = keep.tile([P, PACK, N], BF16, name="w_signed")
+        for t in range(PACK):
+            nc.scalar.activation(w_signed[:, t, :], w_raw[t // 2][:, t % 2, :], ACT.Copy, scale=g_sign[:, t : t + 1])
+        w_grouped = keep.tile([P, N, PACK], BF16, name="w_grouped", align_bytes=64)
+        nc.scalar.copy(w_grouped[:].rearrange("p (c i) t -> p c t i", i=4), w_signed[:].rearrange("p t (c i) -> p c t i", i=4))
+
+        d_picked = keep.tile([P, H], U32, name="d_picked", tag="picked", align_bytes=64)
+        nc.vector.tensor_copy(d_picked[:], d_word_win[:].indirect(kidx_t[:]))
+        key_codes = keep.tile([P, H], U32, name="key_codes", align_bytes=64)
+        nc.vector.tensor_copy(key_codes[:].rearrange("p (t m) -> p m t", t=PACK), d_picked[:].rearrange("p (m t) -> p m t", t=PACK))
+
+        w_codes = keep.tile([P, N], U32, name="w_codes", align_bytes=64)
+        w_scales = keep.tile([P, N], U8, name="w_scales", align_bytes=64)
+
+        nc.vector.quantize_mx(out=w_codes[:].bitcast(FP8X4), scales=w_scales[:], in_=w_grouped[:].rearrange("p m t -> p (m t)"))
+
+        tok_codes = keep.tile([P, S], U32, name="tok_codes", tag="picked", align_bytes=64)
+        banks = []
+        for c in range(CHUNKS):
+            nc.vector.tensor_copy(tok_codes[:, c * TOK : (c + 1) * TOK], x_word_win[:].indirect(offs_t[:, c * TOK // 16 : (c + 1) * TOK // 16]))
+            pair = [psum.tile([P, 2, TOK], F32, name="bank", tag="bank") for h in range(2)]
+            banks.append(pair)
+            for t in range(PACK):
+                nc.tensor.matmul_mx(
+                    out=pair[t // 2][:, t % 2, :],
+                    lhsT=key_codes[:, t * P : (t + 1) * P].bitcast(FP8X4),
+                    lhsT_scale=key_scales[:, t * P : (t + 1) * P],
+                    rhs=tok_codes[:, c * TOK : (c + 1) * TOK].bitcast(FP8X4),
+                    rhs_scale=tok_scales[:, c * TOK : (c + 1) * TOK],
+                    start=True,
+                    stop=True,
+                )
+
+        out_view = out.rearrange("(j p) v -> p j v", p=P)
+        both = [keep.tile([P, PACK, 2, len(g) * PAS], BF16, name="both%d" % n) for n, g in enumerate(GROUPS)]
+
+        def weigh(n, c, on_vector):
+            v0 = (c - GROUPS[n][0]) * PAS
+            for t in range(PACK):
+                scores = banks[c][t // 2][:, t % 2, :].rearrange("p (v e) -> p e v", e=2)
+                if on_vector[t // 2]:
+                    nc.vector.tensor_scalar(both[n][:, t, :, v0 : v0 + PAS], scores, g_size[:, t : t + 1], None, ALU.mult)
+                else:
+                    nc.scalar.activation(both[n][:, t, :, v0 : v0 + PAS], scores, ACT.Copy, scale=g_size[:, t : t + 1])
+
+        def pool_and_quantize(n):
+            width = len(GROUPS[n]) * PAS
+            z_grouped = keep.tile([P, width, PACK], BF16, name="z_grouped%d" % n, align_bytes=64)
+            nc.vector.tensor_tensor(
+                z_grouped[:].rearrange("p (c i) t -> p c t i", i=4),
+                both[n][:, :, 0, :].rearrange("p t (c i) -> p c t i", i=4),
+                both[n][:, :, 1, :].rearrange("p t (c i) -> p c t i", i=4),
+                ALU.max,
+            )
+            z_codes = keep.tile([P, width], U32, name="z_codes%d" % n, align_bytes=64)
+            z_scales = keep.tile([P, width], U8, name="z_scales%d" % n, align_bytes=64)
+            nc.vector.quantize_mx(out=z_codes[:].bitcast(FP8X4), scales=z_scales[:], in_=z_grouped[:].rearrange("p v t -> p (v t)"))
+            return z_codes, z_scales
+
+        def values(n, z_codes, z_scales, on_vector):
+            width = len(GROUPS[n]) * PAS
+            v0 = GROUPS[n][0] * PAS
+            for h in range(2):
+                acc = psum.tile([P, 2, TOK], F32, name="bank", tag="bank")
+                for j in range(2):
+                    m0 = (2 * h + j) * P
+                    nc.tensor.matmul_mx(
+                        out=acc[:, j, 0:width],
+                        lhsT=w_codes[:, m0 : m0 + P].bitcast(FP8X4),
+                        lhsT_scale=w_scales[:, m0 : m0 + P],
+                        rhs=z_codes[:].bitcast(FP8X4),
+                        rhs_scale=z_scales[:],
+                        start=True,
+                        stop=True,
+                    )
+                res = keep.tile([P, 2, width], F32, name="res%d_%d" % (n, h))
+                if on_vector[h]:
+                    nc.vector.tensor_copy(res[:], acc[:, :, 0:width])
+                else:
+                    nc.scalar.copy(res[:], acc[:, :, 0:width])
+                nc.sync.dma_start(out=out_view[:, 2 * h : 2 * h + 2, v0 : v0 + width], in_=res[:])
+
+        weigh(0, 0, (False, False))
+        weigh(1, 1, (False, False))
+        weigh(2, 2, (False, False))
+        z0 = pool_and_quantize(0)
+        weigh(3, 3, (False, True))
+        z1 = pool_and_quantize(1)
+        z2 = pool_and_quantize(2)
+        z3 = pool_and_quantize(3)
+        values(0, z0[0], z0[1], (False, False))
+        values(1, z1[0], z1[1], (False, False))
+        values(2, z2[0], z2[1], (False, True))
+        values(3, z3[0], z3[1], (False, True))

@@ -31,25 +31,26 @@ def tile_picked_scorepool_none_p_kernel(tc, x_words, x_scales, d_words, d_scales
 
         kidx_t = keep.tile([P, H // 16], U16, name="kidx_t")
         offs_t = keep.tile([P, S // 16], U16, name="offs_t")
-        d_word_win = keep.tile([P, G], U32, name="d_word_win", align_bytes=64)
+        d_word_win = keep.tile([P, G], U32, name="d_word_win", tag="d_words", align_bytes=64)
         x_word_win = keep.tile([P, T], U32, name="x_word_win", align_bytes=64)
         d_byte_win = keep.tile([P, G], U8, name="d_byte_win", align_bytes=64)
         x_byte_win = keep.tile([P, T], U8, name="x_byte_win", align_bytes=64)
-        w_raw = [keep.tile([P, 2, N], F32, name="w_raw%d" % h) for h in range(2)]
+        w_first = keep.tile([P, PACK - 1, N], F32, name="w_first")
+        w_last = keep.tile([P, N], F32, name="w_last")
         gn_t = keep.tile([P, PACK], F32, name="gn_t")
 
-        nc.vector.memset(d_byte_win[:].bitcast(I32), 0)
         nc.vector.memset(x_byte_win[:].bitcast(I32), 0)
+        nc.vector.memset(d_byte_win[:].bitcast(I32), 0)
 
         w_view = w1.rearrange("(p t) m -> p t m", t=PACK)
-        nc.sync.dma_start(kidx_t[:], kidx)
         nc.sync.dma_start(offs_t[:], offs)
+        nc.sync.dma_start(kidx_t[:], kidx)
         nc.sync.dma_start(out=gn_t[:], in_=gn.rearrange("(p t) o -> p (t o)", t=PACK))
-        nc.sync.dma_start(out=d_byte_win[0:P:8, :].bitcast(I32), in_=d_scales[0].bitcast(I32))
-        for h in range(2):
-            nc.sync.dma_start(out=w_raw[h][:], in_=w_view[:, 2 * h : 2 * h + 2, :])
         for r in range(4):
             nc.sync.dma_start(out=x_byte_win[r:P:32, :].bitcast(I32), in_=x_scales[0, r:16:4, :].bitcast(I32))
+        nc.sync.dma_start(out=w_first[:], in_=w_view[:, 0 : PACK - 1, :])
+        nc.sync.dma_start(out=d_byte_win[0:P:8, :].bitcast(I32), in_=d_scales[0].bitcast(I32))
+        nc.sync.dma_start(out=w_last[:], in_=w_view[:, PACK - 1, :])
         nc.sync.dma_start(out=d_word_win[:].bitcast(I32), in_=d_words[0].rearrange("p n t -> p (n t)").bitcast(I32))
         nc.sync.dma_start(out=x_word_win[:].bitcast(I32), in_=x_words[0].rearrange("p n t -> p (n t)").bitcast(I32))
 
@@ -58,6 +59,9 @@ def tile_picked_scorepool_none_p_kernel(tc, x_words, x_scales, d_words, d_scales
         nc.scalar.activation(g_sign[:], gn_t[:], ACT.Sign)
         nc.scalar.activation(g_size[:], gn_t[:], ACT.Abs, scale=0.0625)
 
+        tok_scales = keep.tile([P, S], U8, name="tok_scales", align_bytes=64)
+        nc.vector.tensor_copy(tok_scales[:], x_byte_win[:].indirect(offs_t[:]))
+
         d_bytes = keep.tile([P, H], U8, name="d_bytes", align_bytes=64)
         nc.vector.tensor_copy(d_bytes[:], d_byte_win[:].indirect(kidx_t[:]))
         key_scales = keep.tile([P, H], U8, name="key_scales", align_bytes=64)
@@ -65,12 +69,9 @@ def tile_picked_scorepool_none_p_kernel(tc, x_words, x_scales, d_words, d_scales
         for r in range(1, 4):
             nc.sync.dma_start(out=key_scales[r:P:32, :].bitcast(I32), in_=key_scales[8 * r : P : 32, :].bitcast(I32))
 
-        tok_scales = keep.tile([P, S], U8, name="tok_scales", align_bytes=64)
-        nc.vector.tensor_copy(tok_scales[:], x_byte_win[:].indirect(offs_t[:]))
-
         w_signed = keep.tile([P, PACK, N], BF16, name="w_signed")
         for t in range(PACK):
-            nc.scalar.activation(w_signed[:, t, :], w_raw[t // 2][:, t % 2, :], ACT.Copy, scale=g_sign[:, t : t + 1])
+            nc.scalar.activation(w_signed[:, t, :], w_first[:, t, :] if t < PACK - 1 else w_last[:], ACT.Copy, scale=g_sign[:, t : t + 1])
         w_grouped = keep.tile([P, N, PACK], BF16, name="w_grouped", align_bytes=64)
         nc.scalar.copy(w_grouped[:].rearrange("p (c i) t -> p c t i", i=4), w_signed[:].rearrange("p t (c i) -> p c t i", i=4))
 
@@ -79,7 +80,7 @@ def tile_picked_scorepool_none_p_kernel(tc, x_words, x_scales, d_words, d_scales
         key_codes = keep.tile([P, H], U32, name="key_codes", align_bytes=64)
         nc.vector.tensor_copy(key_codes[:].rearrange("p (t m) -> p m t", t=PACK), d_picked[:].rearrange("p (m t) -> p m t", t=PACK))
 
-        w_codes = keep.tile([P, N], U32, name="w_codes", align_bytes=64)
+        w_codes = keep.tile([P, N], U32, name="w_codes", tag="d_words", align_bytes=64)
         w_scales = keep.tile([P, N], U8, name="w_scales", align_bytes=64)
 
         nc.vector.quantize_mx(out=w_codes[:].bitcast(FP8X4), scales=w_scales[:], in_=w_grouped[:].rearrange("p m t -> p (m t)"))
@@ -152,13 +153,13 @@ def tile_picked_scorepool_none_p_kernel(tc, x_words, x_scales, d_words, d_scales
 
         weigh(0, 0, (False, False))
         weigh(1, 1, (False, False))
-        weigh(2, 2, (False, False))
         z0 = pool_and_quantize(0)
-        weigh(3, 3, (False, True))
+        weigh(2, 2, (False, False))
         z1 = pool_and_quantize(1)
+        weigh(3, 3, (False, True))
         z2 = pool_and_quantize(2)
         z3 = pool_and_quantize(3)
         values(0, z0[0], z0[1], (False, False))
         values(1, z1[0], z1[1], (False, False))
-        values(2, z2[0], z2[1], (False, True))
+        values(2, z2[0], z2[1], (False, False))
         values(3, z3[0], z3[1], (False, True))

@@ -20,7 +20,7 @@ PACK = 4
 CHUNKS = 4
 TOK = S // CHUNKS
 PAS = V // CHUNKS
-GROUPS = ((0,), (1,), (2,), (3,))
+BANK_GROUPS = (((0,), (1,), (2, 3)), ((0, 1), (2, 3)))
 
 
 def tile_picked_scorepool_none_p_kernel(tc, x_words, x_scales, d_words, d_scales, gn, w1, offs, kidx, out):
@@ -31,26 +31,25 @@ def tile_picked_scorepool_none_p_kernel(tc, x_words, x_scales, d_words, d_scales
 
         kidx_t = keep.tile([P, H // 16], U16, name="kidx_t")
         offs_t = keep.tile([P, S // 16], U16, name="offs_t")
-        d_word_win = keep.tile([P, G], U32, name="d_word_win", tag="d_words", align_bytes=64)
-        x_word_win = keep.tile([P, T], U32, name="x_word_win", align_bytes=64)
+        d_word_win = keep.tile([P, G], U32, name="d_word_win", align_bytes=64)
+        x_word_win = keep.tile([P, T], U32, name="x_word_win", tag="x_words", align_bytes=64)
         d_byte_win = keep.tile([P, G], U8, name="d_byte_win", align_bytes=64)
         x_byte_win = keep.tile([P, T], U8, name="x_byte_win", align_bytes=64)
-        w_first = keep.tile([P, PACK - 1, N], F32, name="w_first")
-        w_last = keep.tile([P, N], F32, name="w_last")
+        w_first = keep.tile([P, N], F32, name="w_first")
+        w_rest = keep.tile([P, PACK - 1, N], F32, name="w_rest")
         gn_t = keep.tile([P, PACK], F32, name="gn_t")
 
-        nc.vector.memset(x_byte_win[:].bitcast(I32), 0)
         nc.vector.memset(d_byte_win[:].bitcast(I32), 0)
+        nc.vector.memset(x_byte_win[:].bitcast(I32), 0)
 
         w_view = w1.rearrange("(p t) m -> p t m", t=PACK)
-        nc.sync.dma_start(offs_t[:], offs)
         nc.sync.dma_start(kidx_t[:], kidx)
         nc.sync.dma_start(out=gn_t[:], in_=gn.rearrange("(p t) o -> p (t o)", t=PACK))
-        for r in range(4):
-            nc.sync.dma_start(out=x_byte_win[r:P:32, :].bitcast(I32), in_=x_scales[0, r:16:4, :].bitcast(I32))
-        nc.sync.dma_start(out=w_first[:], in_=w_view[:, 0 : PACK - 1, :])
+        nc.sync.dma_start(out=w_first[:], in_=w_view[:, 0, :])
         nc.sync.dma_start(out=d_byte_win[0:P:8, :].bitcast(I32), in_=d_scales[0].bitcast(I32))
-        nc.sync.dma_start(out=w_last[:], in_=w_view[:, PACK - 1, :])
+        nc.sync.dma_start(out=x_byte_win[0:P:8, :].bitcast(I32), in_=x_scales[0].bitcast(I32))
+        nc.sync.dma_start(offs_t[:], offs)
+        nc.sync.dma_start(out=w_rest[:], in_=w_view[:, 1:PACK, :])
         nc.sync.dma_start(out=d_word_win[:].bitcast(I32), in_=d_words[0].rearrange("p n t -> p (n t)").bitcast(I32))
         nc.sync.dma_start(out=x_word_win[:].bitcast(I32), in_=x_words[0].rearrange("p n t -> p (n t)").bitcast(I32))
 
@@ -59,107 +58,117 @@ def tile_picked_scorepool_none_p_kernel(tc, x_words, x_scales, d_words, d_scales
         nc.scalar.activation(g_sign[:], gn_t[:], ACT.Sign)
         nc.scalar.activation(g_size[:], gn_t[:], ACT.Abs, scale=0.0625)
 
-        tok_scales = keep.tile([P, S], U8, name="tok_scales", align_bytes=64)
-        nc.vector.tensor_copy(tok_scales[:], x_byte_win[:].indirect(offs_t[:]))
-
         d_bytes = keep.tile([P, H], U8, name="d_bytes", align_bytes=64)
         nc.vector.tensor_copy(d_bytes[:], d_byte_win[:].indirect(kidx_t[:]))
-        key_scales = keep.tile([P, H], U8, name="key_scales", align_bytes=64)
-        nc.vector.tensor_copy(key_scales[:].rearrange("p (t m) -> p t m", t=PACK), d_bytes[:].rearrange("p (m t) -> p t m", t=PACK))
+        planes_in = keep.tile([P, H + S], U8, name="planes_in", align_bytes=64)
+        key_scales = planes_in[:, 0:H]
+        tok_scales = planes_in[:, H : H + S]
+        x_bytes = keep.tile([P, S], U8, name="x_bytes", align_bytes=64)
+        nc.vector.tensor_copy(x_bytes[:], x_byte_win[:].indirect(offs_t[:]))
+        nc.vector.tensor_copy(key_scales.rearrange("p (t m) -> p t m", t=PACK), d_bytes[:].rearrange("p (m t) -> p t m", t=PACK))
+        nc.vector.tensor_copy(tok_scales.bitcast(I32), x_bytes[:].bitcast(I32))
         for r in range(1, 4):
-            nc.sync.dma_start(out=key_scales[r:P:32, :].bitcast(I32), in_=key_scales[8 * r : P : 32, :].bitcast(I32))
+            nc.sync.dma_start(out=planes_in[r:P:32, :].bitcast(I32), in_=planes_in[8 * r : P : 32, :].bitcast(I32))
 
         w_signed = keep.tile([P, PACK, N], BF16, name="w_signed")
         for t in range(PACK):
-            nc.scalar.activation(w_signed[:, t, :], w_first[:, t, :] if t < PACK - 1 else w_last[:], ACT.Copy, scale=g_sign[:, t : t + 1])
-        w_grouped = keep.tile([P, N, PACK], BF16, name="w_grouped", align_bytes=64)
+            nc.scalar.activation(w_signed[:, t, :], w_rest[:, t - 1, :] if t else w_first[:], ACT.Copy, scale=g_sign[:, t : t + 1])
+        w_grouped = keep.tile([P, N, PACK], BF16, name="w_grouped", tag="w_grouped", align_bytes=64)
         nc.scalar.copy(w_grouped[:].rearrange("p (c i) t -> p c t i", i=4), w_signed[:].rearrange("p t (c i) -> p c t i", i=4))
 
         d_picked = keep.tile([P, H], U32, name="d_picked", tag="picked", align_bytes=64)
         nc.vector.tensor_copy(d_picked[:], d_word_win[:].indirect(kidx_t[:]))
+
         key_codes = keep.tile([P, H], U32, name="key_codes", align_bytes=64)
         nc.vector.tensor_copy(key_codes[:].rearrange("p (t m) -> p m t", t=PACK), d_picked[:].rearrange("p (m t) -> p m t", t=PACK))
 
-        w_codes = keep.tile([P, N], U32, name="w_codes", tag="d_words", align_bytes=64)
+        tok_codes = keep.tile([P, S], U32, name="tok_codes", tag="picked", align_bytes=64)
+
+        def score(bank, t, j0, width):
+            nc.tensor.matmul_mx(
+                out=bank,
+                lhsT=key_codes[:, t * P : (t + 1) * P].bitcast(FP8X4),
+                lhsT_scale=key_scales[:, t * P : (t + 1) * P],
+                rhs=tok_codes[:, j0 : j0 + width].bitcast(FP8X4),
+                rhs_scale=tok_scales[:, j0 : j0 + width],
+                start=True,
+                stop=True,
+            )
+
+        banks = []
+        for c in range(CHUNKS):
+            nc.vector.tensor_copy(tok_codes[:, c * TOK : (c + 1) * TOK], x_word_win[:].indirect(offs_t[:, c * TOK // 16 : (c + 1) * TOK // 16]))
+            tiles = []
+            for group in BANK_GROUPS[min(c, 1)]:
+                bank = psum.tile([P, 2 * TOK], F32, name="bank", tag="bank")
+                for n, t in enumerate(group):
+                    tiles.append(bank[:, n * TOK : (n + 1) * TOK])
+                    score(tiles[t], t, c * TOK, TOK)
+            banks.append(tiles)
+
+        w_codes = keep.tile([P, N], U32, name="w_codes", tag="x_words", align_bytes=64)
         w_scales = keep.tile([P, N], U8, name="w_scales", align_bytes=64)
 
         nc.vector.quantize_mx(out=w_codes[:].bitcast(FP8X4), scales=w_scales[:], in_=w_grouped[:].rearrange("p m t -> p (m t)"))
 
-        tok_codes = keep.tile([P, S], U32, name="tok_codes", tag="picked", align_bytes=64)
-        banks = []
-        for c in range(CHUNKS):
-            nc.vector.tensor_copy(tok_codes[:, c * TOK : (c + 1) * TOK], x_word_win[:].indirect(offs_t[:, c * TOK // 16 : (c + 1) * TOK // 16]))
-            pair = [psum.tile([P, 2, TOK], F32, name="bank", tag="bank") for h in range(2)]
-            banks.append(pair)
+        out_view = out.rearrange("(j p) v -> p j v", p=P)
+        z_grouped = [keep.tile([P, PAS, PACK], BF16, name="z_grouped%d" % c, align_bytes=64) for c in range(CHUNKS)]
+        planes = [keep.tile([P, PACK, 2, PAS], BF16, name="planes%d" % c) for c in range(CHUNKS)]
+
+        def weigh(c):
             for t in range(PACK):
+                nc.scalar.activation(planes[c][:, t, :, :], banks[c][t].rearrange("p (v e) -> p e v", e=2), ACT.Copy, scale=g_size[:, t : t + 1])
+
+        def pool(c):
+            nc.vector.tensor_tensor(
+                z_grouped[c][:].rearrange("p (c i) t -> p c t i", i=4),
+                planes[c][:, :, 0, :].rearrange("p t (c i) -> p c t i", i=4),
+                planes[c][:, :, 1, :].rearrange("p t (c i) -> p c t i", i=4),
+                ALU.max,
+            )
+
+        z_codes = [keep.tile([P, PAS], U32, name="z_codes%d" % c, align_bytes=64) for c in range(CHUNKS)]
+        z_scales = [keep.tile([P, PAS], U8, name="z_scales%d" % c, align_bytes=64) for c in range(CHUNKS)]
+
+        def quantize(c):
+            nc.vector.quantize_mx(out=z_codes[c][:].bitcast(FP8X4), scales=z_scales[c][:], in_=z_grouped[c][:].rearrange("p v t -> p (v t)"))
+
+        def values(c, j0, count, on_vector):
+            acc = psum.tile([P, 2 * TOK], F32, name="bank", tag="bank")
+            for j in range(count):
+                m0 = (j0 + j) * P
                 nc.tensor.matmul_mx(
-                    out=pair[t // 2][:, t % 2, :],
-                    lhsT=key_codes[:, t * P : (t + 1) * P].bitcast(FP8X4),
-                    lhsT_scale=key_scales[:, t * P : (t + 1) * P],
-                    rhs=tok_codes[:, c * TOK : (c + 1) * TOK].bitcast(FP8X4),
-                    rhs_scale=tok_scales[:, c * TOK : (c + 1) * TOK],
+                    out=acc[:, j * PAS : (j + 1) * PAS],
+                    lhsT=w_codes[:, m0 : m0 + P].bitcast(FP8X4),
+                    lhsT_scale=w_scales[:, m0 : m0 + P],
+                    rhs=z_codes[c][:].bitcast(FP8X4),
+                    rhs_scale=z_scales[c][:],
                     start=True,
                     stop=True,
                 )
+            res = keep.tile([P, count, PAS], F32, name="res%d_%d" % (c, j0))
+            sums = acc[:, 0 : count * PAS].rearrange("p (j v) -> p j v", j=count)
+            place = out_view[:, j0 : j0 + count, c * PAS : (c + 1) * PAS]
+            if on_vector:
+                nc.vector.tensor_copy(res[:], sums)
+            else:
+                nc.scalar.copy(res[:], sums)
+            nc.sync.dma_start(out=place, in_=res[:])
 
-        out_view = out.rearrange("(j p) v -> p j v", p=P)
-        both = [keep.tile([P, PACK, 2, len(g) * PAS], BF16, name="both%d" % n) for n, g in enumerate(GROUPS)]
-
-        def weigh(n, c, on_vector):
-            v0 = (c - GROUPS[n][0]) * PAS
-            for t in range(PACK):
-                scores = banks[c][t // 2][:, t % 2, :].rearrange("p (v e) -> p e v", e=2)
-                if on_vector[t // 2]:
-                    nc.vector.tensor_scalar(both[n][:, t, :, v0 : v0 + PAS], scores, g_size[:, t : t + 1], None, ALU.mult)
-                else:
-                    nc.scalar.activation(both[n][:, t, :, v0 : v0 + PAS], scores, ACT.Copy, scale=g_size[:, t : t + 1])
-
-        def pool_and_quantize(n):
-            width = len(GROUPS[n]) * PAS
-            z_grouped = keep.tile([P, width, PACK], BF16, name="z_grouped%d" % n, align_bytes=64)
-            nc.vector.tensor_tensor(
-                z_grouped[:].rearrange("p (c i) t -> p c t i", i=4),
-                both[n][:, :, 0, :].rearrange("p t (c i) -> p c t i", i=4),
-                both[n][:, :, 1, :].rearrange("p t (c i) -> p c t i", i=4),
-                ALU.max,
-            )
-            z_codes = keep.tile([P, width], U32, name="z_codes%d" % n, align_bytes=64)
-            z_scales = keep.tile([P, width], U8, name="z_scales%d" % n, align_bytes=64)
-            nc.vector.quantize_mx(out=z_codes[:].bitcast(FP8X4), scales=z_scales[:], in_=z_grouped[:].rearrange("p v t -> p (v t)"))
-            return z_codes, z_scales
-
-        def values(n, z_codes, z_scales, on_vector):
-            width = len(GROUPS[n]) * PAS
-            v0 = GROUPS[n][0] * PAS
-            for h in range(2):
-                acc = psum.tile([P, 2, TOK], F32, name="bank", tag="bank")
-                for j in range(2):
-                    m0 = (2 * h + j) * P
-                    nc.tensor.matmul_mx(
-                        out=acc[:, j, 0:width],
-                        lhsT=w_codes[:, m0 : m0 + P].bitcast(FP8X4),
-                        lhsT_scale=w_scales[:, m0 : m0 + P],
-                        rhs=z_codes[:].bitcast(FP8X4),
-                        rhs_scale=z_scales[:],
-                        start=True,
-                        stop=True,
-                    )
-                res = keep.tile([P, 2, width], F32, name="res%d_%d" % (n, h))
-                if on_vector[h]:
-                    nc.vector.tensor_copy(res[:], acc[:, :, 0:width])
-                else:
-                    nc.scalar.copy(res[:], acc[:, :, 0:width])
-                nc.sync.dma_start(out=out_view[:, 2 * h : 2 * h + 2, v0 : v0 + width], in_=res[:])
-
-        weigh(0, 0, (False, False))
-        weigh(1, 1, (False, False))
-        z0 = pool_and_quantize(0)
-        weigh(2, 2, (False, False))
-        z1 = pool_and_quantize(1)
-        weigh(3, 3, (False, True))
-        z2 = pool_and_quantize(2)
-        z3 = pool_and_quantize(3)
-        values(0, z0[0], z0[1], (False, False))
-        values(1, z1[0], z1[1], (False, False))
-        values(2, z2[0], z2[1], (False, False))
-        values(3, z3[0], z3[1], (False, True))
+        for c in range(CHUNKS):
+            weigh(c)
+        pool(0)
+        quantize(0)
+        pool(1)
+        values(0, 0, 2, True)
+        values(0, 2, 2, True)
+        quantize(1)
+        pool(2)
+        quantize(2)
+        pool(3)
+        quantize(3)
+        for c in (1, 2):
+            values(c, 0, 2, False)
+            values(c, 2, 2, False)
+        values(3, 0, 2, False)
+        values(3, 2, 2, True)

@@ -20,6 +20,7 @@ PACK = 4
 CHUNKS = 4
 TOK = S // CHUNKS
 PAS = V // CHUNKS
+HALF = N // 2
 BANK_GROUPS = (((0,), (1,), (2, 3)), ((0, 1), (2, 3)))
 
 
@@ -43,10 +44,10 @@ def tile_picked_scorepool_none_p_kernel(tc, x_words, x_scales, d_words, d_scales
         nc.vector.memset(x_byte_win[:].bitcast(I32), 0)
 
         w_view = w1.rearrange("(p t) m -> p t m", t=PACK)
-        nc.sync.dma_start(kidx_t[:], kidx)
-        nc.sync.dma_start(out=gn_t[:], in_=gn.rearrange("(p t) o -> p (t o)", t=PACK))
         nc.sync.dma_start(out=w_first[:], in_=w_view[:, 0, :])
+        nc.sync.dma_start(kidx_t[:], kidx)
         nc.sync.dma_start(out=d_byte_win[0:P:8, :].bitcast(I32), in_=d_scales[0].bitcast(I32))
+        nc.sync.dma_start(out=gn_t[:], in_=gn.rearrange("(p t) o -> p (t o)", t=PACK))
         nc.sync.dma_start(out=x_byte_win[0:P:8, :].bitcast(I32), in_=x_scales[0].bitcast(I32))
         nc.sync.dma_start(offs_t[:], offs)
         nc.sync.dma_start(out=w_rest[:], in_=w_view[:, 1:PACK, :])
@@ -73,13 +74,23 @@ def tile_picked_scorepool_none_p_kernel(tc, x_words, x_scales, d_words, d_scales
         w_signed = keep.tile([P, PACK, N], BF16, name="w_signed")
         for t in range(PACK):
             nc.scalar.activation(w_signed[:, t, :], w_rest[:, t - 1, :] if t else w_first[:], ACT.Copy, scale=g_sign[:, t : t + 1])
-        w_grouped = keep.tile([P, N, PACK], BF16, name="w_grouped", tag="w_grouped", align_bytes=64)
-        nc.scalar.copy(w_grouped[:].rearrange("p (c i) t -> p c t i", i=4), w_signed[:].rearrange("p t (c i) -> p c t i", i=4))
+        w_grouped = [keep.tile([P, HALF, PACK], BF16, name="w_grouped%d" % h, tag="w_grouped%d" % h, align_bytes=64) for h in range(2)]
+        for h in range(2):
+            nc.scalar.copy(w_grouped[h][:].rearrange("p (c i) t -> p c t i", i=4), w_signed[:, :, h * HALF : (h + 1) * HALF].rearrange("p t (c i) -> p c t i", i=4))
+        w_codes = [
+            keep.tile([P, HALF], U32, name="w_codes0", align_bytes=64),
+            keep.tile([P, HALF], U32, name="w_codes1", tag="x_words", align_bytes=64),
+        ]
+        w_scales = [keep.tile([P, HALF], U8, name="w_scales%d" % h, align_bytes=64) for h in range(2)]
+
+        def quantize_w(h):
+            nc.vector.quantize_mx(out=w_codes[h][:].bitcast(FP8X4), scales=w_scales[h][:], in_=w_grouped[h][:].rearrange("p m t -> p (m t)"))
 
         d_picked = keep.tile([P, H], U32, name="d_picked", tag="picked", align_bytes=64)
         nc.vector.tensor_copy(d_picked[:], d_word_win[:].indirect(kidx_t[:]))
+        quantize_w(0)
 
-        key_codes = keep.tile([P, H], U32, name="key_codes", align_bytes=64)
+        key_codes = keep.tile([P, H], U32, name="key_codes", tag="w_grouped0", align_bytes=64)
         nc.vector.tensor_copy(key_codes[:].rearrange("p (t m) -> p m t", t=PACK), d_picked[:].rearrange("p (m t) -> p m t", t=PACK))
 
         tok_codes = keep.tile([P, S], U32, name="tok_codes", tag="picked", align_bytes=64)
@@ -106,10 +117,7 @@ def tile_picked_scorepool_none_p_kernel(tc, x_words, x_scales, d_words, d_scales
                     score(tiles[t], t, c * TOK, TOK)
             banks.append(tiles)
 
-        w_codes = keep.tile([P, N], U32, name="w_codes", tag="x_words", align_bytes=64)
-        w_scales = keep.tile([P, N], U8, name="w_scales", align_bytes=64)
-
-        nc.vector.quantize_mx(out=w_codes[:].bitcast(FP8X4), scales=w_scales[:], in_=w_grouped[:].rearrange("p m t -> p (m t)"))
+        quantize_w(1)
 
         out_view = out.rearrange("(j p) v -> p j v", p=P)
         z_grouped = [keep.tile([P, PAS, PACK], BF16, name="z_grouped%d" % c, align_bytes=64) for c in range(CHUNKS)]
@@ -136,11 +144,11 @@ def tile_picked_scorepool_none_p_kernel(tc, x_words, x_scales, d_words, d_scales
         def values(c, j0, count, on_vector):
             acc = psum.tile([P, 2 * TOK], F32, name="bank", tag="bank")
             for j in range(count):
-                m0 = (j0 + j) * P
+                m0 = j * P
                 nc.tensor.matmul_mx(
                     out=acc[:, j * PAS : (j + 1) * PAS],
-                    lhsT=w_codes[:, m0 : m0 + P].bitcast(FP8X4),
-                    lhsT_scale=w_scales[:, m0 : m0 + P],
+                    lhsT=w_codes[j0 // 2][:, m0 : m0 + P].bitcast(FP8X4),
+                    lhsT_scale=w_scales[j0 // 2][:, m0 : m0 + P],
                     rhs=z_codes[c][:].bitcast(FP8X4),
                     rhs_scale=z_scales[c][:],
                     start=True,

@@ -21,14 +21,19 @@ CHUNKS = 4
 TOK = S // CHUNKS
 PAS = V // CHUNKS
 HALF = N // 2
-BANK_GROUPS = (((0,), (1,), (2, 3)), ((0, 1), (2, 3)))
+BANK_GROUPS = (
+    ((0, (0,)), (1, (1,)), (2, (2, 3))),
+    ((3, (0, 1)), (4, (2, 3))),
+    ((5, (0, 1)), (6, (2, 3))),
+    ((7, (0, 1)), (0, (2,)), (6, (3,))),
+)
 
 
 def tile_picked_scorepool_none_p_kernel(tc, x_words, x_scales, d_words, d_scales, gn, w1, offs, kidx, out):
     nc = tc.nc
     with ExitStack() as ctx:
         keep = ctx.enter_context(tc.tile_pool(name="keep", bufs=1))
-        psum = ctx.enter_context(tc.psum_pool(name="psum", bufs=8))
+        psum = ctx.enter_context(tc.psum_pool(name="psum", bufs=1))
 
         kidx_t = keep.tile([P, H // 16], U16, name="kidx_t")
         offs_t = keep.tile([P, S // 16], U16, name="offs_t")
@@ -37,7 +42,8 @@ def tile_picked_scorepool_none_p_kernel(tc, x_words, x_scales, d_words, d_scales
         d_byte_win = keep.tile([P, G], U8, name="d_byte_win", align_bytes=64)
         x_byte_win = keep.tile([P, T], U8, name="x_byte_win", align_bytes=64)
         w_first = keep.tile([P, N], F32, name="w_first")
-        w_rest = keep.tile([P, PACK - 1, N], F32, name="w_rest")
+        w_second = keep.tile([P, N], F32, name="w_second")
+        w_rest = keep.tile([P, PACK - 2, N], F32, name="w_rest")
         gn_t = keep.tile([P, PACK], F32, name="gn_t")
 
         nc.vector.memset(d_byte_win[:].bitcast(I32), 0)
@@ -47,10 +53,11 @@ def tile_picked_scorepool_none_p_kernel(tc, x_words, x_scales, d_words, d_scales
         nc.sync.dma_start(out=w_first[:], in_=w_view[:, 0, :])
         nc.sync.dma_start(kidx_t[:], kidx)
         nc.sync.dma_start(out=d_byte_win[0:P:8, :].bitcast(I32), in_=d_scales[0].bitcast(I32))
+        nc.sync.dma_start(out=w_second[:], in_=w_view[:, 1, :])
         nc.sync.dma_start(out=gn_t[:], in_=gn.rearrange("(p t) o -> p (t o)", t=PACK))
-        nc.sync.dma_start(out=x_byte_win[0:P:8, :].bitcast(I32), in_=x_scales[0].bitcast(I32))
         nc.sync.dma_start(offs_t[:], offs)
-        nc.sync.dma_start(out=w_rest[:], in_=w_view[:, 1:PACK, :])
+        nc.sync.dma_start(out=x_byte_win[0:P:8, :].bitcast(I32), in_=x_scales[0].bitcast(I32))
+        nc.sync.dma_start(out=w_rest[:], in_=w_view[:, 2:PACK, :])
         nc.sync.dma_start(out=d_word_win[:].bitcast(I32), in_=d_words[0].rearrange("p n t -> p (n t)").bitcast(I32))
         nc.sync.dma_start(out=x_word_win[:].bitcast(I32), in_=x_words[0].rearrange("p n t -> p (n t)").bitcast(I32))
 
@@ -58,6 +65,8 @@ def tile_picked_scorepool_none_p_kernel(tc, x_words, x_scales, d_words, d_scales
         g_sign = keep.tile([P, PACK], F32, name="g_sign")
         nc.scalar.activation(g_sign[:], gn_t[:], ACT.Sign)
         nc.scalar.activation(g_size[:], gn_t[:], ACT.Abs, scale=0.0625)
+        g_early = keep.tile([P, PACK], F32, name="g_early", tag="g_early", align_bytes=64)
+        nc.scalar.activation(g_early[:], gn_t[:], ACT.Abs, scale=0.0625)
 
         d_bytes = keep.tile([P, H], U8, name="d_bytes", align_bytes=64)
         nc.vector.tensor_copy(d_bytes[:], d_byte_win[:].indirect(kidx_t[:]))
@@ -73,13 +82,13 @@ def tile_picked_scorepool_none_p_kernel(tc, x_words, x_scales, d_words, d_scales
 
         w_signed = keep.tile([P, PACK, N], BF16, name="w_signed")
         for t in range(PACK):
-            nc.scalar.activation(w_signed[:, t, :], w_rest[:, t - 1, :] if t else w_first[:], ACT.Copy, scale=g_sign[:, t : t + 1])
+            nc.scalar.activation(w_signed[:, t, :], (w_first[:], w_second[:], w_rest[:, 0, :], w_rest[:, 1, :])[t], ACT.Copy, scale=g_sign[:, t : t + 1])
         w_grouped = [keep.tile([P, HALF, PACK], BF16, name="w_grouped%d" % h, tag="w_grouped%d" % h, align_bytes=64) for h in range(2)]
         for h in range(2):
             nc.scalar.copy(w_grouped[h][:].rearrange("p (c i) t -> p c t i", i=4), w_signed[:, :, h * HALF : (h + 1) * HALF].rearrange("p t (c i) -> p c t i", i=4))
         w_codes = [
             keep.tile([P, HALF], U32, name="w_codes0", align_bytes=64),
-            keep.tile([P, HALF], U32, name="w_codes1", tag="x_words", align_bytes=64),
+            keep.tile([P, HALF], U32, name="w_codes1", tag="g_early", align_bytes=64),
         ]
         w_scales = [keep.tile([P, HALF], U8, name="w_scales%d" % h, align_bytes=64) for h in range(2)]
 
@@ -106,27 +115,36 @@ def tile_picked_scorepool_none_p_kernel(tc, x_words, x_scales, d_words, d_scales
                 stop=True,
             )
 
+        planes = [keep.tile([P, PACK, 2, PAS], BF16, name="planes%d" % c) for c in range(CHUNKS)]
+
+        def weigh(c):
+            for t in range(PACK):
+                scores = banks[c][t].rearrange("p (v e) -> p e v", e=2)
+                if (c, t) == (CHUNKS - 1, PACK - 1):
+                    nc.vector.tensor_scalar_mul(planes[c][:, t, :, :], scores, g_size[:, t : t + 1])
+                elif c * PACK + t <= PACK:
+                    nc.scalar.activation(planes[c][:, t, :, :], scores, ACT.Copy, scale=g_early[:, t : t + 1])
+                else:
+                    nc.scalar.activation(planes[c][:, t, :, :], scores, ACT.Copy, scale=g_size[:, t : t + 1])
+
         banks = []
         for c in range(CHUNKS):
-            nc.vector.tensor_copy(tok_codes[:, c * TOK : (c + 1) * TOK], x_word_win[:].indirect(offs_t[:, c * TOK // 16 : (c + 1) * TOK // 16]))
+            if c < CHUNKS - 1:
+                end = (c + 1) * TOK if c < CHUNKS - 2 else S
+                nc.vector.tensor_copy(tok_codes[:, c * TOK : end], x_word_win[:].indirect(offs_t[:, c * TOK // 16 : end // 16]))
             tiles = []
-            for group in BANK_GROUPS[min(c, 1)]:
-                bank = psum.tile([P, 2 * TOK], F32, name="bank", tag="bank")
+            for slot, group in BANK_GROUPS[c]:
+                bank = psum.tile([P, 2 * TOK], F32, name="bank", tag="bank%d" % slot)
                 for n, t in enumerate(group):
                     tiles.append(bank[:, n * TOK : (n + 1) * TOK])
                     score(tiles[t], t, c * TOK, TOK)
             banks.append(tiles)
+            weigh(c)
 
         quantize_w(1)
 
         out_view = out.rearrange("(j p) v -> p j v", p=P)
         z_grouped = [keep.tile([P, PAS, PACK], BF16, name="z_grouped%d" % c, align_bytes=64) for c in range(CHUNKS)]
-        planes = [keep.tile([P, PACK, 2, PAS], BF16, name="planes%d" % c) for c in range(CHUNKS)]
-
-        def weigh(c):
-            for t in range(PACK):
-                nc.scalar.activation(planes[c][:, t, :, :], banks[c][t].rearrange("p (v e) -> p e v", e=2), ACT.Copy, scale=g_size[:, t : t + 1])
-
         def pool(c):
             nc.vector.tensor_tensor(
                 z_grouped[c][:].rearrange("p (c i) t -> p c t i", i=4),
@@ -141,10 +159,10 @@ def tile_picked_scorepool_none_p_kernel(tc, x_words, x_scales, d_words, d_scales
         def quantize(c):
             nc.vector.quantize_mx(out=z_codes[c][:].bitcast(FP8X4), scales=z_scales[c][:], in_=z_grouped[c][:].rearrange("p v t -> p (v t)"))
 
-        def values(c, j0, count, on_vector):
-            acc = psum.tile([P, 2 * TOK], F32, name="bank", tag="bank")
+        def values(c, j0, count, slot, on_vector):
+            acc = psum.tile([P, 2 * TOK], F32, name="bank", tag="bank%d" % slot)
             for j in range(count):
-                m0 = j * P
+                m0 = (j0 + j) * P % HALF
                 nc.tensor.matmul_mx(
                     out=acc[:, j * PAS : (j + 1) * PAS],
                     lhsT=w_codes[j0 // 2][:, m0 : m0 + P].bitcast(FP8X4),
@@ -163,20 +181,19 @@ def tile_picked_scorepool_none_p_kernel(tc, x_words, x_scales, d_words, d_scales
                 nc.scalar.copy(res[:], sums)
             nc.sync.dma_start(out=place, in_=res[:])
 
-        for c in range(CHUNKS):
-            weigh(c)
         pool(0)
         quantize(0)
         pool(1)
-        values(0, 0, 2, True)
-        values(0, 2, 2, True)
+        values(0, 0, 2, 1, True)
         quantize(1)
         pool(2)
         quantize(2)
         pool(3)
         quantize(3)
-        for c in (1, 2):
-            values(c, 0, 2, False)
-            values(c, 2, 2, False)
-        values(3, 0, 2, False)
-        values(3, 2, 2, True)
+        values(0, 2, 2, 2, False)
+        values(1, 0, 2, 3, False)
+        values(1, 2, 2, 4, False)
+        values(2, 0, 2, 5, False)
+        values(2, 2, 2, 1, False)
+        for j, slot in enumerate((7, 0, 2, 6)):
+            values(3, j, 1, slot, j % 2 == 1)

@@ -139,7 +139,8 @@ def tile_picked_scorepool_none_p_kernel(tc, x_words, x_scales, d_words, d_scales
                     tiles.append(bank[:, n * TOK : (n + 1) * TOK])
                     score(tiles[t], t, c * TOK, TOK)
             banks.append(tiles)
-            weigh(c)
+            if c < CHUNKS - 1:
+                weigh(c)
 
         quantize_w(1)
 
@@ -185,12 +186,13 @@ def tile_picked_scorepool_none_p_kernel(tc, x_words, x_scales, d_words, d_scales
         quantize(0)
         pool(1)
         values(0, 0, 2, 1, True)
+        values(0, 2, 2, 2, False)
+        weigh(CHUNKS - 1)
         quantize(1)
         pool(2)
         quantize(2)
         pool(3)
         quantize(3)
-        values(0, 2, 2, 2, False)
         values(1, 0, 2, 3, False)
         values(1, 2, 2, 4, False)
         values(2, 0, 2, 5, False)

@@ -102,7 +102,7 @@ def tile_picked_scorepool_none_p_kernel(tc, x_words, x_scales, d_words, d_scales
         key_codes = keep.tile([P, H], U32, name="key_codes", tag="w_grouped0", align_bytes=64)
         nc.vector.tensor_copy(key_codes[:].rearrange("p (t m) -> p m t", t=PACK), d_picked[:].rearrange("p (m t) -> p m t", t=PACK))
 
-        tok_codes = keep.tile([P, S], U32, name="tok_codes", tag="picked", align_bytes=64)
+        tok_codes = keep.tile([P, S], U32, name="tok_codes", align_bytes=64)
 
         def score(bank, t, j0, width):
             nc.tensor.matmul_mx(

@@ -53,8 +53,8 @@ def tile_picked_scorepool_none_p_kernel(tc, x_words, x_scales, d_words, d_scales
         nc.sync.dma_start(out=w_first[:], in_=w_view[:, 0, :])
         nc.sync.dma_start(kidx_t[:], kidx)
         nc.sync.dma_start(out=d_byte_win[0:P:8, :].bitcast(I32), in_=d_scales[0].bitcast(I32))
-        nc.sync.dma_start(out=w_second[:], in_=w_view[:, 1, :])
         nc.sync.dma_start(out=gn_t[:], in_=gn.rearrange("(p t) o -> p (t o)", t=PACK))
+        nc.sync.dma_start(out=w_second[:], in_=w_view[:, 1, :])
         nc.sync.dma_start(offs_t[:], offs)
         nc.sync.dma_start(out=x_byte_win[0:P:8, :].bitcast(I32), in_=x_scales[0].bitcast(I32))
         nc.sync.dma_start(out=w_rest[:], in_=w_view[:, 2:PACK, :])

@@ -21,6 +21,7 @@ CHUNKS = 4
 TOK = S // CHUNKS
 PAS = V // CHUNKS
 HALF = N // 2
+EARLY = N - P
 BANK_GROUPS = (
     ((0, (0,)), (1, (1,)), (2, (2, 3))),
     ((3, (0, 1)), (4, (2, 3))),
@@ -41,23 +42,21 @@ def tile_picked_scorepool_none_p_kernel(tc, x_words, x_scales, d_words, d_scales
         x_word_win = keep.tile([P, T], U32, name="x_word_win", tag="x_words", align_bytes=64)
         d_byte_win = keep.tile([P, G], U8, name="d_byte_win", align_bytes=64)
         x_byte_win = keep.tile([P, T], U8, name="x_byte_win", align_bytes=64)
-        w_first = keep.tile([P, N], F32, name="w_first")
-        w_second = keep.tile([P, N], F32, name="w_second")
-        w_rest = keep.tile([P, PACK - 2, N], F32, name="w_rest")
+        w_first = keep.tile([P, EARLY], F32, name="w_first")
+        w_rest = keep.tile([P, PACK - 1, EARLY], F32, name="w_rest")
         gn_t = keep.tile([P, PACK], F32, name="gn_t")
 
         nc.vector.memset(d_byte_win[:].bitcast(I32), 0)
         nc.vector.memset(x_byte_win[:].bitcast(I32), 0)
 
         w_view = w1.rearrange("(p t) m -> p t m", t=PACK)
-        nc.sync.dma_start(out=w_first[:], in_=w_view[:, 0, :])
+        nc.sync.dma_start(out=w_first[:], in_=w_view[:, 0, 0:EARLY])
         nc.sync.dma_start(kidx_t[:], kidx)
         nc.sync.dma_start(out=d_byte_win[0:P:8, :].bitcast(I32), in_=d_scales[0].bitcast(I32))
         nc.sync.dma_start(out=gn_t[:], in_=gn.rearrange("(p t) o -> p (t o)", t=PACK))
-        nc.sync.dma_start(out=w_second[:], in_=w_view[:, 1, :])
+        nc.sync.dma_start(out=w_rest[:], in_=w_view[:, 1:PACK, 0:EARLY])
         nc.sync.dma_start(offs_t[:], offs)
         nc.sync.dma_start(out=x_byte_win[0:P:8, :].bitcast(I32), in_=x_scales[0].bitcast(I32))
-        nc.sync.dma_start(out=w_rest[:], in_=w_view[:, 2:PACK, :])
         nc.sync.dma_start(out=d_word_win[:].bitcast(I32), in_=d_words[0].rearrange("p n t -> p (n t)").bitcast(I32))
         nc.sync.dma_start(out=x_word_win[:].bitcast(I32), in_=x_words[0].rearrange("p n t -> p (n t)").bitcast(I32))
 
@@ -80,12 +79,12 @@ def tile_picked_scorepool_none_p_kernel(tc, x_words, x_scales, d_words, d_scales
         for r in range(1, 4):
             nc.sync.dma_start(out=planes_in[r:P:32, :].bitcast(I32), in_=planes_in[8 * r : P : 32, :].bitcast(I32))
 
-        w_signed = keep.tile([P, PACK, N], BF16, name="w_signed")
+        w_signed = keep.tile([P, PACK, EARLY], BF16, name="w_signed")
         for t in range(PACK):
-            nc.scalar.activation(w_signed[:, t, :], (w_first[:], w_second[:], w_rest[:, 0, :], w_rest[:, 1, :])[t], ACT.Copy, scale=g_sign[:, t : t + 1])
+            nc.scalar.activation(w_signed[:, t, :], w_rest[:, t - 1, :] if t else w_first[:], ACT.Copy, scale=g_sign[:, t : t + 1])
         w_grouped = [keep.tile([P, HALF, PACK], BF16, name="w_grouped%d" % h, tag="w_grouped%d" % h, align_bytes=64) for h in range(2)]
-        for h in range(2):
-            nc.scalar.copy(w_grouped[h][:].rearrange("p (c i) t -> p c t i", i=4), w_signed[:, :, h * HALF : (h + 1) * HALF].rearrange("p t (c i) -> p c t i", i=4))
+        for h, width in enumerate((HALF, EARLY - HALF)):
+            nc.scalar.copy(w_grouped[h][:, 0:width, :].rearrange("p (c i) t -> p c t i", i=4), w_signed[:, :, h * HALF : h * HALF + width].rearrange("p t (c i) -> p c t i", i=4))
         w_codes = [
             keep.tile([P, HALF], U32, name="w_codes0", align_bytes=64),
             keep.tile([P, HALF], U32, name="w_codes1", tag="g_early", align_bytes=64),
@@ -101,6 +100,9 @@ def tile_picked_scorepool_none_p_kernel(tc, x_words, x_scales, d_words, d_scales
 
         key_codes = keep.tile([P, H], U32, name="key_codes", tag="w_grouped0", align_bytes=64)
         nc.vector.tensor_copy(key_codes[:].rearrange("p (t m) -> p m t", t=PACK), d_picked[:].rearrange("p (m t) -> p m t", t=PACK))
+
+        w_late = keep.tile([P, PACK, P], F32, name="w_late", tag="picked", align_bytes=64)
+        nc.sync.dma_start(out=w_late[:], in_=w_view[:, :, EARLY:N])
 
         tok_codes = keep.tile([P, S], U32, name="tok_codes", align_bytes=64)
 
@@ -142,6 +144,12 @@ def tile_picked_scorepool_none_p_kernel(tc, x_words, x_scales, d_words, d_scales
             if c < CHUNKS - 1:
                 weigh(c)
 
+        nc.vector.tensor_tensor(
+            w_grouped[1][:, EARLY - HALF : HALF, :].rearrange("p (c i) t -> p c t i", i=4),
+            w_late[:].rearrange("p t (c i) -> p c t i", i=4),
+            g_sign[:].rearrange("p (a t b) -> p a t b", a=1, b=1).to_broadcast([P, P // 4, PACK, 4]),
+            ALU.mult,
+        )
         quantize_w(1)
 
         out_view = out.rearrange("(j p) v -> p j v", p=P)

@@ -46,17 +46,17 @@ def tile_picked_scorepool_none_p_kernel(tc, x_words, x_scales, d_words, d_scales
         w_rest = keep.tile([P, PACK - 1, EARLY], F32, name="w_rest")
         gn_t = keep.tile([P, PACK], F32, name="gn_t")
 
-        nc.vector.memset(d_byte_win[:].bitcast(I32), 0)
         nc.vector.memset(x_byte_win[:].bitcast(I32), 0)
+        nc.vector.memset(d_byte_win[:].bitcast(I32), 0)
 
         w_view = w1.rearrange("(p t) m -> p t m", t=PACK)
         nc.sync.dma_start(out=w_first[:], in_=w_view[:, 0, 0:EARLY])
-        nc.sync.dma_start(kidx_t[:], kidx)
-        nc.sync.dma_start(out=d_byte_win[0:P:8, :].bitcast(I32), in_=d_scales[0].bitcast(I32))
-        nc.sync.dma_start(out=gn_t[:], in_=gn.rearrange("(p t) o -> p (t o)", t=PACK))
-        nc.sync.dma_start(out=w_rest[:], in_=w_view[:, 1:PACK, 0:EARLY])
         nc.sync.dma_start(offs_t[:], offs)
         nc.sync.dma_start(out=x_byte_win[0:P:8, :].bitcast(I32), in_=x_scales[0].bitcast(I32))
+        nc.sync.dma_start(out=gn_t[:], in_=gn.rearrange("(p t) o -> p (t o)", t=PACK))
+        nc.sync.dma_start(out=w_rest[:], in_=w_view[:, 1:PACK, 0:EARLY])
+        nc.sync.dma_start(kidx_t[:], kidx)
+        nc.sync.dma_start(out=d_byte_win[0:P:8, :].bitcast(I32), in_=d_scales[0].bitcast(I32))
         nc.sync.dma_start(out=d_word_win[:].bitcast(I32), in_=d_words[0].rearrange("p n t -> p (n t)").bitcast(I32))
         nc.sync.dma_start(out=x_word_win[:].bitcast(I32), in_=x_words[0].rearrange("p n t -> p (n t)").bitcast(I32))
 
@@ -67,15 +67,15 @@ def tile_picked_scorepool_none_p_kernel(tc, x_words, x_scales, d_words, d_scales
         g_early = keep.tile([P, PACK], F32, name="g_early", tag="g_early", align_bytes=64)
         nc.scalar.activation(g_early[:], gn_t[:], ACT.Abs, scale=0.0625)
 
+        x_bytes = keep.tile([P, S], U8, name="x_bytes", align_bytes=64)
+        nc.vector.tensor_copy(x_bytes[:], x_byte_win[:].indirect(offs_t[:]))
         d_bytes = keep.tile([P, H], U8, name="d_bytes", align_bytes=64)
         nc.vector.tensor_copy(d_bytes[:], d_byte_win[:].indirect(kidx_t[:]))
         planes_in = keep.tile([P, H + S], U8, name="planes_in", align_bytes=64)
         key_scales = planes_in[:, 0:H]
         tok_scales = planes_in[:, H : H + S]
-        x_bytes = keep.tile([P, S], U8, name="x_bytes", align_bytes=64)
-        nc.vector.tensor_copy(x_bytes[:], x_byte_win[:].indirect(offs_t[:]))
-        nc.vector.tensor_copy(key_scales.rearrange("p (t m) -> p t m", t=PACK), d_bytes[:].rearrange("p (m t) -> p t m", t=PACK))
         nc.vector.tensor_copy(tok_scales.bitcast(I32), x_bytes[:].bitcast(I32))
+        nc.vector.tensor_copy(key_scales.rearrange("p (t m) -> p t m", t=PACK), d_bytes[:].rearrange("p (m t) -> p t m", t=PACK))
         for r in range(1, 4):
             nc.sync.dma_start(out=planes_in[r:P:32, :].bitcast(I32), in_=planes_in[8 * r : P : 32, :].bitcast(I32))
 

@@ -98,7 +98,7 @@ def tile_picked_scorepool_none_p_kernel(tc, x_words, x_scales, d_words, d_scales
         nc.vector.tensor_copy(d_picked[:], d_word_win[:].indirect(kidx_t[:]))
         quantize_w(0)
 
-        key_codes = keep.tile([P, H], U32, name="key_codes", tag="w_grouped0", align_bytes=64)
+        key_codes = keep.tile([P, H], U32, name="key_codes", align_bytes=64)
         nc.vector.tensor_copy(key_codes[:].rearrange("p (t m) -> p m t", t=PACK), d_picked[:].rearrange("p (m t) -> p m t", t=PACK))
 
         w_late = keep.tile([P, PACK, P], F32, name="w_late", tag="picked", align_bytes=64)

@@ -22,6 +22,7 @@ TOK = S // CHUNKS
 PAS = V // CHUNKS
 HALF = N // 2
 EARLY = N - P
+GATHERS = (((0, P), (P, TOK)), ((TOK, 2 * TOK),), ((2 * TOK, S),), ())
 BANK_GROUPS = (
     ((0, (0,)), (1, (1,)), (2, (2, 3))),
     ((3, (0, 1)), (4, (2, 3))),
@@ -121,6 +122,11 @@ def tile_picked_scorepool_none_p_kernel(tc, x_words, x_scales, d_words, d_scales
 
         def weigh(c):
             for t in range(PACK):
+                if (c, t) == (0, 0):
+                    for part in range(2):
+                        scores = banks[c][t][part].rearrange("p (v e) -> p e v", e=2)
+                        nc.scalar.activation(planes[c][:, t, :, part * PAS // 2 : (part + 1) * PAS // 2], scores, ACT.Copy, scale=g_early[:, t : t + 1])
+                    continue
                 scores = banks[c][t].rearrange("p (v e) -> p e v", e=2)
                 if (c, t) == (CHUNKS - 1, PACK - 1):
                     nc.vector.tensor_scalar_mul(planes[c][:, t, :, :], scores, g_size[:, t : t + 1])
@@ -131,12 +137,18 @@ def tile_picked_scorepool_none_p_kernel(tc, x_words, x_scales, d_words, d_scales
 
         banks = []
         for c in range(CHUNKS):
-            if c < CHUNKS - 1:
-                end = (c + 1) * TOK if c < CHUNKS - 2 else S
-                nc.vector.tensor_copy(tok_codes[:, c * TOK : end], x_word_win[:].indirect(offs_t[:, c * TOK // 16 : end // 16]))
+            for start, end in GATHERS[c]:
+                nc.vector.tensor_copy(tok_codes[:, start:end], x_word_win[:].indirect(offs_t[:, start // 16 : end // 16]))
             tiles = []
             for slot, group in BANK_GROUPS[c]:
                 bank = psum.tile([P, 2 * TOK], F32, name="bank", tag="bank%d" % slot)
+                if (c, slot) == (0, 0):
+                    tiles.append([bank[:, 0:P]])
+                    score(tiles[0][0], 0, 0, P)
+                    continue
+                if (c, slot) == (0, 1):
+                    tiles[0].append(bank[:, TOK : TOK + P])
+                    score(tiles[0][1], 0, P, P)
                 for n, t in enumerate(group):
                     tiles.append(bank[:, n * TOK : (n + 1) * TOK])
                     score(tiles[t], t, c * TOK, TOK)

@@ -24,10 +24,10 @@ HALF = N // 2
 EARLY = N - P
 GATHERS = (((0, P), (P, TOK)), ((TOK, 2 * TOK),), ((2 * TOK, S),), ())
 BANK_GROUPS = (
-    ((0, (0,)), (1, (1,)), (2, (2, 3))),
-    ((3, (0, 1)), (4, (2, 3))),
-    ((5, (0, 1)), (6, (2, 3))),
-    ((7, (0, 1)), (0, (2,)), (6, (3,))),
+    ((2, (1,)), (3, (2,)), (4, (3,))),
+    ((5, (0,)), (6, (1,)), (7, (2,)), (0, (3,))),
+    ((1, (0,)), (2, (1,)), (3, (2,)), (4, (3,))),
+    ((5, (0, 1)), (6, (2,)), (4, (3,))),
 )
 
 
@@ -70,7 +70,7 @@ def tile_picked_scorepool_none_p_kernel(tc, x_words, x_scales, d_words, d_scales
 
         x_bytes = keep.tile([P, S], U8, name="x_bytes", align_bytes=64)
         nc.vector.tensor_copy(x_bytes[:], x_byte_win[:].indirect(offs_t[:]))
-        d_bytes = keep.tile([P, H], U8, name="d_bytes", align_bytes=64)
+        d_bytes = keep.tile([P, H], U8, name="d_bytes", tag="d_bytes", align_bytes=64)
         nc.vector.tensor_copy(d_bytes[:], d_byte_win[:].indirect(kidx_t[:]))
         planes_in = keep.tile([P, H + S], U8, name="planes_in", align_bytes=64)
         key_scales = planes_in[:, 0:H]
@@ -102,7 +102,7 @@ def tile_picked_scorepool_none_p_kernel(tc, x_words, x_scales, d_words, d_scales
         key_codes = keep.tile([P, H], U32, name="key_codes", align_bytes=64)
         nc.vector.tensor_copy(key_codes[:].rearrange("p (t m) -> p m t", t=PACK), d_picked[:].rearrange("p (m t) -> p m t", t=PACK))
 
-        w_late = keep.tile([P, PACK, P], F32, name="w_late", tag="picked", align_bytes=64)
+        w_late = keep.tile([P, PACK, P], F32, name="w_late", tag="d_bytes", align_bytes=64)
         nc.sync.dma_start(out=w_late[:], in_=w_view[:, :, EARLY:N])
 
         tok_codes = keep.tile([P, S], U32, name="tok_codes", align_bytes=64)
@@ -140,15 +140,12 @@ def tile_picked_scorepool_none_p_kernel(tc, x_words, x_scales, d_words, d_scales
             for start, end in GATHERS[c]:
                 nc.vector.tensor_copy(tok_codes[:, start:end], x_word_win[:].indirect(offs_t[:, start // 16 : end // 16]))
             tiles = []
+            if c == 0:
+                tiles.append([psum.tile([P, 2 * TOK], F32, name="bank", tag="bank%d" % part)[:, 0:P] for part in range(2)])
+                for part in range(2):
+                    score(tiles[0][part], 0, part * P, P)
             for slot, group in BANK_GROUPS[c]:
                 bank = psum.tile([P, 2 * TOK], F32, name="bank", tag="bank%d" % slot)
-                if (c, slot) == (0, 0):
-                    tiles.append([bank[:, 0:P]])
-                    score(tiles[0][0], 0, 0, P)
-                    continue
-                if (c, slot) == (0, 1):
-                    tiles[0].append(bank[:, TOK : TOK + P])
-                    score(tiles[0][1], 0, P, P)
                 for n, t in enumerate(group):
                     tiles.append(bank[:, n * TOK : (n + 1) * TOK])
                     score(tiles[t], t, c * TOK, TOK)
@@ -205,17 +202,17 @@ def tile_picked_scorepool_none_p_kernel(tc, x_words, x_scales, d_words, d_scales
         pool(0)
         quantize(0)
         pool(1)
-        values(0, 0, 2, 1, True)
-        values(0, 2, 2, 2, False)
+        values(0, 0, 2, 7, True)
+        values(0, 2, 2, 0, False)
         weigh(CHUNKS - 1)
         quantize(1)
         pool(2)
         quantize(2)
         pool(3)
         quantize(3)
-        values(1, 0, 2, 3, False)
-        values(1, 2, 2, 4, False)
-        values(2, 0, 2, 5, False)
-        values(2, 2, 2, 1, False)
-        for j, slot in enumerate((7, 0, 2, 6)):
+        values(1, 0, 2, 1, False)
+        values(1, 2, 2, 2, False)
+        values(2, 0, 2, 3, False)
+        values(2, 2, 2, 7, False)
+        for j, slot in enumerate((5, 6, 0, 4)):
             values(3, j, 1, slot, j % 2 == 1)

@@ -104,6 +104,12 @@ def tile_picked_scorepool_none_p_kernel(tc, x_words, x_scales, d_words, d_scales
 
         w_late = keep.tile([P, PACK, P], F32, name="w_late", tag="d_bytes", align_bytes=64)
         nc.sync.dma_start(out=w_late[:], in_=w_view[:, :, EARLY:N])
+        nc.gpsimd.tensor_tensor(
+            w_grouped[1][:, EARLY - HALF : HALF, :],
+            w_late[:].rearrange("p t m -> p m t"),
+            g_sign[:].rearrange("p (a t) -> p a t", a=1).to_broadcast([P, P, PACK]),
+            ALU.mult,
+        )
 
         tok_codes = keep.tile([P, S], U32, name="tok_codes", align_bytes=64)
 
@@ -128,9 +134,9 @@ def tile_picked_scorepool_none_p_kernel(tc, x_words, x_scales, d_words, d_scales
                         nc.scalar.activation(planes[c][:, t, :, part * PAS // 2 : (part + 1) * PAS // 2], scores, ACT.Copy, scale=g_early[:, t : t + 1])
                     continue
                 scores = banks[c][t].rearrange("p (v e) -> p e v", e=2)
-                if (c, t) == (CHUNKS - 1, PACK - 1):
+                if (c, t) in ((1, 0), (CHUNKS - 1, PACK - 1)):
                     nc.vector.tensor_scalar_mul(planes[c][:, t, :, :], scores, g_size[:, t : t + 1])
-                elif c * PACK + t <= PACK:
+                elif c * PACK + t <= PACK + 1:
                     nc.scalar.activation(planes[c][:, t, :, :], scores, ACT.Copy, scale=g_early[:, t : t + 1])
                 else:
                     nc.scalar.activation(planes[c][:, t, :, :], scores, ACT.Copy, scale=g_size[:, t : t + 1])
@@ -152,14 +158,6 @@ def tile_picked_scorepool_none_p_kernel(tc, x_words, x_scales, d_words, d_scales
             banks.append(tiles)
             if c < CHUNKS - 1:
                 weigh(c)
-
-        nc.vector.tensor_tensor(
-            w_grouped[1][:, EARLY - HALF : HALF, :].rearrange("p (c i) t -> p c t i", i=4),
-            w_late[:].rearrange("p t (c i) -> p c t i", i=4),
-            g_sign[:].rearrange("p (a t b) -> p a t b", a=1, b=1).to_broadcast([P, P // 4, PACK, 4]),
-            ALU.mult,
-        )
-        quantize_w(1)
 
         out_view = out.rearrange("(j p) v -> p j v", p=P)
         z_grouped = [keep.tile([P, PAS, PACK], BF16, name="z_grouped%d" % c, align_bytes=64) for c in range(CHUNKS)]
@@ -200,6 +198,7 @@ def tile_picked_scorepool_none_p_kernel(tc, x_words, x_scales, d_words, d_scales
             nc.sync.dma_start(out=place, in_=res[:])
 
         pool(0)
+        quantize_w(1)
         quantize(0)
         pool(1)
         values(0, 0, 2, 7, True)

@@ -22,13 +22,10 @@ TOK = S // CHUNKS
 PAS = V // CHUNKS
 HALF = N // 2
 EARLY = N - P
-GATHERS = (((0, P), (P, TOK)), ((TOK, 2 * TOK),), ((2 * TOK, S),), ())
-BANK_GROUPS = (
-    ((2, (1,)), (3, (2,)), (4, (3,))),
-    ((5, (0,)), (6, (1,)), (7, (2,)), (0, (3,))),
-    ((1, (0,)), (2, (1,)), (3, (2,)), (4, (3,))),
-    ((5, (0, 1)), (6, (2,)), (4, (3,))),
-)
+BANK = 512
+LINE = 256
+SCORE_BANKS = ((0, 2, 3, 4), (5, 6, 7, 0), (1, 2, 3, 4), (5, 5, 6, 4))
+VECTOR_READS = ((1, 0), (3, 3))
 
 
 def tile_picked_scorepool_none_p_kernel(tc, x_words, x_scales, d_words, d_scales, gn, w1, offs, kidx, out):
@@ -39,16 +36,18 @@ def tile_picked_scorepool_none_p_kernel(tc, x_words, x_scales, d_words, d_scales
 
         kidx_t = keep.tile([P, H // 16], U16, name="kidx_t")
         offs_t = keep.tile([P, S // 16], U16, name="offs_t")
-        d_word_win = keep.tile([P, G], U32, name="d_word_win", align_bytes=64)
-        x_word_win = keep.tile([P, T], U32, name="x_word_win", tag="x_words", align_bytes=64)
-        d_byte_win = keep.tile([P, G], U8, name="d_byte_win", align_bytes=64)
-        x_byte_win = keep.tile([P, T], U8, name="x_byte_win", align_bytes=64)
-        w_first = keep.tile([P, EARLY], F32, name="w_first")
-        w_rest = keep.tile([P, PACK - 1, EARLY], F32, name="w_rest")
+        d_word_win = keep.tile([P, G], U32, name="d_word_win", align_bytes=LINE)
+        x_word_win = keep.tile([P, T], U32, name="x_word_win", align_bytes=LINE)
+        d_byte_win = keep.tile([P, G], U8, name="d_byte_win", align_bytes=LINE)
+        x_byte_win = keep.tile([P, T], U8, name="x_byte_win", align_bytes=LINE)
+        placed = keep.tile([P, S + H], U8, name="placed", align_bytes=LINE)
+        w_first = keep.tile([P, EARLY], F32, name="w_first", align_bytes=LINE)
+        w_rest = keep.tile([P, PACK - 1, EARLY], F32, name="w_rest", align_bytes=LINE)
         gn_t = keep.tile([P, PACK], F32, name="gn_t")
 
         nc.vector.memset(x_byte_win[:].bitcast(I32), 0)
         nc.vector.memset(d_byte_win[:].bitcast(I32), 0)
+        nc.vector.memset(placed[:].bitcast(I32), 0)
 
         w_view = w1.rearrange("(p t) m -> p t m", t=PACK)
         nc.sync.dma_start(out=w_first[:], in_=w_view[:, 0, 0:EARLY])
@@ -68,17 +67,12 @@ def tile_picked_scorepool_none_p_kernel(tc, x_words, x_scales, d_words, d_scales
         g_early = keep.tile([P, PACK], F32, name="g_early", tag="g_early", align_bytes=64)
         nc.scalar.activation(g_early[:], gn_t[:], ACT.Abs, scale=0.0625)
 
-        x_bytes = keep.tile([P, S], U8, name="x_bytes", align_bytes=64)
-        nc.vector.tensor_copy(x_bytes[:], x_byte_win[:].indirect(offs_t[:]))
-        d_bytes = keep.tile([P, H], U8, name="d_bytes", tag="d_bytes", align_bytes=64)
-        nc.vector.tensor_copy(d_bytes[:], d_byte_win[:].indirect(kidx_t[:]))
-        planes_in = keep.tile([P, H + S], U8, name="planes_in", align_bytes=64)
-        key_scales = planes_in[:, 0:H]
-        tok_scales = planes_in[:, H : H + S]
-        nc.vector.tensor_copy(tok_scales.bitcast(I32), x_bytes[:].bitcast(I32))
-        nc.vector.tensor_copy(key_scales.rearrange("p (t m) -> p t m", t=PACK), d_bytes[:].rearrange("p (m t) -> p t m", t=PACK))
-        for r in range(1, 4):
-            nc.sync.dma_start(out=planes_in[r:P:32, :].bitcast(I32), in_=planes_in[8 * r : P : 32, :].bitcast(I32))
+        picked_bytes = keep.tile([P, S + H], U8, name="picked_bytes", tag="picked_bytes", align_bytes=LINE)
+        nc.vector.tensor_copy(picked_bytes[:, 0:S], x_byte_win[:].indirect(offs_t[:]))
+        nc.vector.tensor_copy(picked_bytes[:, S : S + H], d_byte_win[:].indirect(kidx_t[:]))
+        for r in range(4):
+            nc.sync.dma_start(out=placed[r:P:32, :].bitcast(I32), in_=picked_bytes[8 * r : P : 32, :].bitcast(I32))
+        tok_scales = placed[:, 0:S]
 
         w_signed = keep.tile([P, PACK, EARLY], BF16, name="w_signed")
         for t in range(PACK):
@@ -86,23 +80,76 @@ def tile_picked_scorepool_none_p_kernel(tc, x_words, x_scales, d_words, d_scales
         w_grouped = [keep.tile([P, HALF, PACK], BF16, name="w_grouped%d" % h, tag="w_grouped%d" % h, align_bytes=64) for h in range(2)]
         for h, width in enumerate((HALF, EARLY - HALF)):
             nc.scalar.copy(w_grouped[h][:, 0:width, :].rearrange("p (c i) t -> p c t i", i=4), w_signed[:, :, h * HALF : h * HALF + width].rearrange("p t (c i) -> p c t i", i=4))
-        w_codes = [
-            keep.tile([P, HALF], U32, name="w_codes0", align_bytes=64),
-            keep.tile([P, HALF], U32, name="w_codes1", tag="g_early", align_bytes=64),
-        ]
+        w_codes = [keep.tile([P, HALF], U32, name="w_codes0", align_bytes=64)]
         w_scales = [keep.tile([P, HALF], U8, name="w_scales%d" % h, align_bytes=64) for h in range(2)]
 
         def quantize_w(h):
             nc.vector.quantize_mx(out=w_codes[h][:].bitcast(FP8X4), scales=w_scales[h][:], in_=w_grouped[h][:].rearrange("p m t -> p (m t)"))
 
-        d_picked = keep.tile([P, H], U32, name="d_picked", tag="picked", align_bytes=64)
+        d_picked = keep.tile([P, H], U32, name="d_picked", tag="picked", align_bytes=LINE)
         nc.vector.tensor_copy(d_picked[:], d_word_win[:].indirect(kidx_t[:]))
         quantize_w(0)
 
         key_codes = keep.tile([P, H], U32, name="key_codes", align_bytes=64)
         nc.vector.tensor_copy(key_codes[:].rearrange("p (t m) -> p m t", t=PACK), d_picked[:].rearrange("p (m t) -> p m t", t=PACK))
 
-        w_late = keep.tile([P, PACK, P], F32, name="w_late", tag="d_bytes", align_bytes=64)
+        tok_first = keep.tile([P, TOK], U32, name="tok_first", align_bytes=64)
+        tok_rest = keep.tile([P, S - TOK], U32, name="tok_rest", tag="picked_bytes", align_bytes=LINE)
+
+        def tok_codes(j0, j1):
+            return tok_first[:, j0:j1] if j0 < TOK else tok_rest[:, j0 - TOK : j1 - TOK]
+
+        def gather_tokens(j0, j1):
+            nc.vector.tensor_copy(tok_codes(j0, j1), x_word_win[:].indirect(offs_t[:, j0 // 16 : j1 // 16]))
+
+        key_scales = keep.tile([P, H], U8, name="key_scales", align_bytes=64)
+        dealt = key_scales[:].rearrange("p (t m) -> p t m", t=PACK)
+        undealt = placed[:, S : S + H].rearrange("p (m t) -> p t m", t=PACK)
+        gather_tokens(0, TOK)
+        nc.vector.tensor_copy(dealt, undealt)
+
+        def score(dst, t, j0, j1):
+            nc.tensor.matmul_mx(
+                out=dst,
+                lhsT=key_codes[:, t * P : (t + 1) * P].bitcast(FP8X4),
+                lhsT_scale=key_scales[:, t * P : (t + 1) * P],
+                rhs=tok_codes(j0, j1).bitcast(FP8X4),
+                rhs_scale=tok_scales[:, j0:j1],
+                start=True,
+                stop=True,
+            )
+
+        def bank(slot):
+            return psum.tile([P, BANK], F32, name="bank", tag="bank%d" % slot)
+
+        planes = [keep.tile([P, PACK, 2, PAS], BF16, name="planes%d" % c) for c in range(CHUNKS)]
+
+        def weigh(c, t, scores):
+            pairs = scores.rearrange("p (v e) -> p e v", e=2)
+            if (c, t) in VECTOR_READS:
+                nc.vector.tensor_scalar_mul(planes[c][:, t, :, :], pairs, g_size[:, t : t + 1])
+            else:
+                n = c * PACK + t
+                weight = g_early if n <= PACK + 1 else g_size
+                nc.scalar.activation(planes[c][:, t, :, :], pairs, ACT.Copy, scale=weight[:, t : t + 1])
+
+        def score_chunk(c):
+            tiles = []
+            for t in range(PACK):
+                if t and SCORE_BANKS[c][t] == SCORE_BANKS[c][t - 1]:
+                    tiles.append(whole[:, TOK : 2 * TOK])
+                else:
+                    whole = bank(SCORE_BANKS[c][t])
+                    tiles.append(whole[:, 0:TOK])
+                score(tiles[t], t, c * TOK, (c + 1) * TOK)
+            return tiles
+
+        def weigh_chunk(c, tiles):
+            for t in range(PACK):
+                weigh(c, t, tiles[t])
+
+        weigh_chunk(0, score_chunk(0))
+        w_late = keep.tile([P, PACK, P], F32, name="w_late", tag="picked", align_bytes=LINE)
         nc.sync.dma_start(out=w_late[:], in_=w_view[:, :, EARLY:N])
         nc.gpsimd.tensor_tensor(
             w_grouped[1][:, EARLY - HALF : HALF, :],
@@ -110,54 +157,12 @@ def tile_picked_scorepool_none_p_kernel(tc, x_words, x_scales, d_words, d_scales
             g_sign[:].rearrange("p (a t) -> p a t", a=1).to_broadcast([P, P, PACK]),
             ALU.mult,
         )
-
-        tok_codes = keep.tile([P, S], U32, name="tok_codes", align_bytes=64)
-
-        def score(bank, t, j0, width):
-            nc.tensor.matmul_mx(
-                out=bank,
-                lhsT=key_codes[:, t * P : (t + 1) * P].bitcast(FP8X4),
-                lhsT_scale=key_scales[:, t * P : (t + 1) * P],
-                rhs=tok_codes[:, j0 : j0 + width].bitcast(FP8X4),
-                rhs_scale=tok_scales[:, j0 : j0 + width],
-                start=True,
-                stop=True,
-            )
-
-        planes = [keep.tile([P, PACK, 2, PAS], BF16, name="planes%d" % c) for c in range(CHUNKS)]
-
-        def weigh(c):
-            for t in range(PACK):
-                if (c, t) == (0, 0):
-                    for part in range(2):
-                        scores = banks[c][t][part].rearrange("p (v e) -> p e v", e=2)
-                        nc.scalar.activation(planes[c][:, t, :, part * PAS // 2 : (part + 1) * PAS // 2], scores, ACT.Copy, scale=g_early[:, t : t + 1])
-                    continue
-                scores = banks[c][t].rearrange("p (v e) -> p e v", e=2)
-                if (c, t) in ((1, 0), (CHUNKS - 1, PACK - 1)):
-                    nc.vector.tensor_scalar_mul(planes[c][:, t, :, :], scores, g_size[:, t : t + 1])
-                elif c * PACK + t <= PACK + 1:
-                    nc.scalar.activation(planes[c][:, t, :, :], scores, ACT.Copy, scale=g_early[:, t : t + 1])
-                else:
-                    nc.scalar.activation(planes[c][:, t, :, :], scores, ACT.Copy, scale=g_size[:, t : t + 1])
-
-        banks = []
-        for c in range(CHUNKS):
-            for start, end in GATHERS[c]:
-                nc.vector.tensor_copy(tok_codes[:, start:end], x_word_win[:].indirect(offs_t[:, start // 16 : end // 16]))
-            tiles = []
-            if c == 0:
-                tiles.append([psum.tile([P, 2 * TOK], F32, name="bank", tag="bank%d" % part)[:, 0:P] for part in range(2)])
-                for part in range(2):
-                    score(tiles[0][part], 0, part * P, P)
-            for slot, group in BANK_GROUPS[c]:
-                bank = psum.tile([P, 2 * TOK], F32, name="bank", tag="bank%d" % slot)
-                for n, t in enumerate(group):
-                    tiles.append(bank[:, n * TOK : (n + 1) * TOK])
-                    score(tiles[t], t, c * TOK, TOK)
-            banks.append(tiles)
-            if c < CHUNKS - 1:
-                weigh(c)
+        gather_tokens(TOK, 2 * TOK)
+        weigh_chunk(1, score_chunk(1))
+        w_codes.append(keep.tile([P, HALF], U32, name="w_codes1", tag="g_early", align_bytes=64))
+        gather_tokens(2 * TOK, S)
+        weigh_chunk(2, score_chunk(2))
+        last_tiles = score_chunk(3)
 
         out_view = out.rearrange("(j p) v -> p j v", p=P)
         z_grouped = [keep.tile([P, PAS, PACK], BF16, name="z_grouped%d" % c, align_bytes=64) for c in range(CHUNKS)]
@@ -176,7 +181,7 @@ def tile_picked_scorepool_none_p_kernel(tc, x_words, x_scales, d_words, d_scales
             nc.vector.quantize_mx(out=z_codes[c][:].bitcast(FP8X4), scales=z_scales[c][:], in_=z_grouped[c][:].rearrange("p v t -> p (v t)"))
 
         def values(c, j0, count, slot, on_vector):
-            acc = psum.tile([P, 2 * TOK], F32, name="bank", tag="bank%d" % slot)
+            acc = bank(slot)
             for j in range(count):
                 m0 = (j0 + j) * P % HALF
                 nc.tensor.matmul_mx(
@@ -188,7 +193,7 @@ def tile_picked_scorepool_none_p_kernel(tc, x_words, x_scales, d_words, d_scales
                     start=True,
                     stop=True,
                 )
-            res = keep.tile([P, count, PAS], F32, name="res%d_%d" % (c, j0))
+            res = keep.tile([P, count, PAS], F32, name="res%d_%d" % (c, j0), align_bytes=LINE)
             sums = acc[:, 0 : count * PAS].rearrange("p (j v) -> p j v", j=count)
             place = out_view[:, j0 : j0 + count, c * PAS : (c + 1) * PAS]
             if on_vector:
@@ -203,7 +208,7 @@ def tile_picked_scorepool_none_p_kernel(tc, x_words, x_scales, d_words, d_scales
         pool(1)
         values(0, 0, 2, 7, True)
         values(0, 2, 2, 0, False)
-        weigh(CHUNKS - 1)
+        weigh_chunk(3, last_tiles)
         quantize(1)
         pool(2)
         quantize(2)

@@ -36,7 +36,7 @@ def tile_picked_scorepool_none_p_kernel(tc, x_words, x_scales, d_words, d_scales
 
         kidx_t = keep.tile([P, H // 16], U16, name="kidx_t")
         offs_t = keep.tile([P, S // 16], U16, name="offs_t")
-        d_word_win = keep.tile([P, G], U32, name="d_word_win", align_bytes=LINE)
+        d_word_win = keep.tile([P, G], U32, name="d_word_win", tag="d_word_win", align_bytes=LINE)
         x_word_win = keep.tile([P, T], U32, name="x_word_win", align_bytes=LINE)
         d_byte_win = keep.tile([P, G], U8, name="d_byte_win", align_bytes=LINE)
         x_byte_win = keep.tile([P, T], U8, name="x_byte_win", align_bytes=LINE)
@@ -106,7 +106,8 @@ def tile_picked_scorepool_none_p_kernel(tc, x_words, x_scales, d_words, d_scales
         dealt = key_scales[:].rearrange("p (t m) -> p t m", t=PACK)
         undealt = placed[:, S : S + H].rearrange("p (m t) -> p t m", t=PACK)
         gather_tokens(0, TOK)
-        nc.vector.tensor_copy(dealt, undealt)
+        for t0 in (0, PACK // 2):
+            nc.vector.tensor_copy(dealt[:, t0 : t0 + PACK // 2, :], undealt[:, t0 : t0 + PACK // 2, :])
 
         def score(dst, t, j0, j1):
             nc.tensor.matmul_mx(
@@ -149,7 +150,7 @@ def tile_picked_scorepool_none_p_kernel(tc, x_words, x_scales, d_words, d_scales
                 weigh(c, t, tiles[t])
 
         weigh_chunk(0, score_chunk(0))
-        w_late = keep.tile([P, PACK, P], F32, name="w_late", tag="picked", align_bytes=LINE)
+        w_late = keep.tile([P, PACK, P], F32, name="w_late", tag="d_word_win", align_bytes=LINE)
         nc.sync.dma_start(out=w_late[:], in_=w_view[:, :, EARLY:N])
         nc.gpsimd.tensor_tensor(
             w_grouped[1][:, EARLY - HALF : HALF, :],

@@ -21,7 +21,7 @@ CHUNKS = 4
 TOK = S // CHUNKS
 PAS = V // CHUNKS
 HALF = N // 2
-EARLY = N - P
+EARLY = 11 * N // 16
 BANK = 512
 LINE = 256
 SCORE_BANKS = ((0, 2, 3, 4), (5, 6, 7, 0), (1, 2, 3, 4), (5, 5, 6, 4))
@@ -53,8 +53,8 @@ def tile_picked_scorepool_none_p_kernel(tc, x_words, x_scales, d_words, d_scales
         nc.sync.dma_start(out=w_first[:], in_=w_view[:, 0, 0:EARLY])
         nc.sync.dma_start(offs_t[:], offs)
         nc.sync.dma_start(out=x_byte_win[0:P:8, :].bitcast(I32), in_=x_scales[0].bitcast(I32))
-        nc.sync.dma_start(out=gn_t[:], in_=gn.rearrange("(p t) o -> p (t o)", t=PACK))
         nc.sync.dma_start(out=w_rest[:], in_=w_view[:, 1:PACK, 0:EARLY])
+        nc.sync.dma_start(out=gn_t[:], in_=gn.rearrange("(p t) o -> p (t o)", t=PACK))
         nc.sync.dma_start(kidx_t[:], kidx)
         nc.sync.dma_start(out=d_byte_win[0:P:8, :].bitcast(I32), in_=d_scales[0].bitcast(I32))
         nc.sync.dma_start(out=d_word_win[:].bitcast(I32), in_=d_words[0].rearrange("p n t -> p (n t)").bitcast(I32))
@@ -150,12 +150,12 @@ def tile_picked_scorepool_none_p_kernel(tc, x_words, x_scales, d_words, d_scales
                 weigh(c, t, tiles[t])
 
         weigh_chunk(0, score_chunk(0))
-        w_late = keep.tile([P, PACK, P], F32, name="w_late", tag="d_word_win", align_bytes=LINE)
+        w_late = keep.tile([P, PACK, N - EARLY], F32, name="w_late", tag="d_word_win", align_bytes=LINE)
         nc.sync.dma_start(out=w_late[:], in_=w_view[:, :, EARLY:N])
         nc.gpsimd.tensor_tensor(
             w_grouped[1][:, EARLY - HALF : HALF, :],
             w_late[:].rearrange("p t m -> p m t"),
-            g_sign[:].rearrange("p (a t) -> p a t", a=1).to_broadcast([P, P, PACK]),
+            g_sign[:].rearrange("p (a t) -> p a t", a=1).to_broadcast([P, N - EARLY, PACK]),
             ALU.mult,
         )
         gather_tokens(TOK, 2 * TOK)

from contextlib import ExitStack

import concourse.mybir as mybir

K, T, S, V, N, G, H = 512, 2048, 1024, 512, 512, 2048, 512
FLOPS = 2 * K * H * S + 2 * H * N * V

F32 = mybir.dt.float32
BF16 = mybir.dt.bfloat16
I32 = mybir.dt.int32
U32 = mybir.dt.uint32
U16 = mybir.dt.uint16
U8 = mybir.dt.uint8
FP8X4 = mybir.dt.float8_e4m3fn_x4
ACT = mybir.ActivationFunctionType
ALU = mybir.AluOpType

P = 128
PACK = 4
CHUNKS = 4
TOK = S // CHUNKS
PAS = V // CHUNKS
HALF = N // 2
EARLY = 11 * N // 16
BANK = 512
LINE = 256
SCORE_BANKS = ((0, 2, 3, 4), (5, 6, 7, 0), (1, 2, 3, 4), (5, 5, 6, 4))
VECTOR_READS = ((1, 0), (3, 3))


def tile_picked_scorepool_none_p_kernel(tc, x_words, x_scales, d_words, d_scales, gn, w1, offs, kidx, out):
    nc = tc.nc
    with ExitStack() as ctx:
        keep = ctx.enter_context(tc.tile_pool(name="keep", bufs=1))
        psum = ctx.enter_context(tc.psum_pool(name="psum", bufs=1))

        kidx_t = keep.tile([P, H // 16], U16, name="kidx_t")
        offs_t = keep.tile([P, S // 16], U16, name="offs_t")
        d_word_win = keep.tile([P, G], U32, name="d_word_win", tag="d_word_win", align_bytes=LINE)
        x_word_win = keep.tile([P, T], U32, name="x_word_win", align_bytes=LINE)
        d_byte_win = keep.tile([P, G], U8, name="d_byte_win", align_bytes=LINE)
        x_byte_win = keep.tile([P, T], U8, name="x_byte_win", align_bytes=LINE)
        placed = keep.tile([P, S + H], U8, name="placed", align_bytes=LINE)
        w_first = keep.tile([P, EARLY], F32, name="w_first", align_bytes=LINE)
        w_rest = keep.tile([P, PACK - 1, EARLY], F32, name="w_rest", align_bytes=LINE)
        gn_t = keep.tile([P, PACK], F32, name="gn_t")

        nc.vector.memset(x_byte_win[:].bitcast(I32), 0)
        nc.vector.memset(d_byte_win[:].bitcast(I32), 0)
        nc.vector.memset(placed[:].bitcast(I32), 0)

        w_view = w1.rearrange("(p t) m -> p t m", t=PACK)
        nc.sync.dma_start(out=w_first[:], in_=w_view[:, 0, 0:EARLY])
        nc.sync.dma_start(offs_t[:], offs)
        nc.sync.dma_start(out=x_byte_win[0:P:8, :].bitcast(I32), in_=x_scales[0].bitcast(I32))
        nc.sync.dma_start(out=w_rest[:], in_=w_view[:, 1:PACK, 0:EARLY])
        nc.sync.dma_start(out=gn_t[:], in_=gn.rearrange("(p t) o -> p (t o)", t=PACK))
        nc.sync.dma_start(kidx_t[:], kidx)
        nc.sync.dma_start(out=d_byte_win[0:P:8, :].bitcast(I32), in_=d_scales[0].bitcast(I32))
        nc.sync.dma_start(out=d_word_win[:].bitcast(I32), in_=d_words[0].rearrange("p n t -> p (n t)").bitcast(I32))
        nc.sync.dma_start(out=x_word_win[:].bitcast(I32), in_=x_words[0].rearrange("p n t -> p (n t)").bitcast(I32))

        g_size = keep.tile([P, PACK], F32, name="g_size")
        g_sign = keep.tile([P, PACK], F32, name="g_sign")
        nc.scalar.activation(g_sign[:], gn_t[:], ACT.Sign)
        nc.scalar.activation(g_size[:], gn_t[:], ACT.Abs, scale=0.0625)
        g_early = keep.tile([P, PACK], F32, name="g_early", tag="g_early", align_bytes=64)
        nc.scalar.activation(g_early[:], gn_t[:], ACT.Abs, scale=0.0625)

        picked_bytes = keep.tile([P, S + H], U8, name="picked_bytes", tag="picked_bytes", align_bytes=LINE)
        nc.vector.tensor_copy(picked_bytes[:, 0:S], x_byte_win[:].indirect(offs_t[:]))
        nc.vector.tensor_copy(picked_bytes[:, S : S + H], d_byte_win[:].indirect(kidx_t[:]))
        for r in range(4):
            nc.sync.dma_start(out=placed[r:P:32, :].bitcast(I32), in_=picked_bytes[8 * r : P : 32, :].bitcast(I32))
        tok_scales = placed[:, 0:S]

        w_signed = keep.tile([P, PACK, EARLY], BF16, name="w_signed")
        for t in range(PACK):
            nc.scalar.activation(w_signed[:, t, :], w_rest[:, t - 1, :] if t else w_first[:], ACT.Copy, scale=g_sign[:, t : t + 1])
        w_grouped = [keep.tile([P, HALF, PACK], BF16, name="w_grouped%d" % h, tag="w_grouped%d" % h, align_bytes=64) for h in range(2)]
        for h, width in enumerate((HALF, EARLY - HALF)):
            nc.scalar.copy(w_grouped[h][:, 0:width, :].rearrange("p (c i) t -> p c t i", i=4), w_signed[:, :, h * HALF : h * HALF + width].rearrange("p t (c i) -> p c t i", i=4))
        w_codes = [keep.tile([P, HALF], U32, name="w_codes0", align_bytes=64)]
        w_scales = [keep.tile([P, HALF], U8, name="w_scales%d" % h, align_bytes=64) for h in range(2)]

        def quantize_w(h):
            nc.vector.quantize_mx(out=w_codes[h][:].bitcast(FP8X4), scales=w_scales[h][:], in_=w_grouped[h][:].rearrange("p m t -> p (m t)"))

        d_picked = keep.tile([P, H], U32, name="d_picked", tag="picked", align_bytes=LINE)
        nc.vector.tensor_copy(d_picked[:], d_word_win[:].indirect(kidx_t[:]))
        quantize_w(0)

        key_codes = keep.tile([P, H], U32, name="key_codes", align_bytes=64)
        nc.vector.tensor_copy(key_codes[:].rearrange("p (t m) -> p m t", t=PACK), d_picked[:].rearrange("p (m t) -> p m t", t=PACK))

        tok_first = keep.tile([P, TOK], U32, name="tok_first", align_bytes=64)
        tok_rest = keep.tile([P, S - TOK], U32, name="tok_rest", tag="picked_bytes", align_bytes=LINE)

        def tok_codes(j0, j1):
            return tok_first[:, j0:j1] if j0 < TOK else tok_rest[:, j0 - TOK : j1 - TOK]

        def gather_tokens(j0, j1):
            nc.vector.tensor_copy(tok_codes(j0, j1), x_word_win[:].indirect(offs_t[:, j0 // 16 : j1 // 16]))

        key_scales = keep.tile([P, H], U8, name="key_scales", align_bytes=64)
        dealt = key_scales[:].rearrange("p (t m) -> p t m", t=PACK)
        undealt = placed[:, S : S + H].rearrange("p (m t) -> p t m", t=PACK)
        gather_tokens(0, TOK)
        for t0 in (0, PACK // 2):
            nc.vector.tensor_copy(dealt[:, t0 : t0 + PACK // 2, :], undealt[:, t0 : t0 + PACK // 2, :])

        def score(dst, t, j0, j1):
            nc.tensor.matmul_mx(
                out=dst,
                lhsT=key_codes[:, t * P : (t + 1) * P].bitcast(FP8X4),
                lhsT_scale=key_scales[:, t * P : (t + 1) * P],
                rhs=tok_codes(j0, j1).bitcast(FP8X4),
                rhs_scale=tok_scales[:, j0:j1],
                start=True,
                stop=True,
            )

        def bank(slot):
            return psum.tile([P, BANK], F32, name="bank", tag="bank%d" % slot)

        planes = [keep.tile([P, PACK, 2, PAS], BF16, name="planes%d" % c) for c in range(CHUNKS)]

        def weigh(c, t, scores):
            pairs = scores.rearrange("p (v e) -> p e v", e=2)
            if (c, t) in VECTOR_READS:
                nc.vector.tensor_scalar_mul(planes[c][:, t, :, :], pairs, g_size[:, t : t + 1])
            else:
                n = c * PACK + t
                weight = g_early if n <= PACK + 1 else g_size
                nc.scalar.activation(planes[c][:, t, :, :], pairs, ACT.Copy, scale=weight[:, t : t + 1])

        def score_chunk(c):
            tiles = []
            for t in range(PACK):
                if t and SCORE_BANKS[c][t] == SCORE_BANKS[c][t - 1]:
                    tiles.append(whole[:, TOK : 2 * TOK])
                else:
                    whole = bank(SCORE_BANKS[c][t])
                    tiles.append(whole[:, 0:TOK])
                score(tiles[t], t, c * TOK, (c + 1) * TOK)
            return tiles

        def weigh_chunk(c, tiles):
            for t in range(PACK):
                weigh(c, t, tiles[t])

        weigh_chunk(0, score_chunk(0))
        w_late = keep.tile([P, PACK, N - EARLY], F32, name="w_late", tag="d_word_win", align_bytes=LINE)
        nc.sync.dma_start(out=w_late[:], in_=w_view[:, :, EARLY:N])
        nc.gpsimd.tensor_tensor(
            w_grouped[1][:, EARLY - HALF : HALF, :],
            w_late[:].rearrange("p t m -> p m t"),
            g_sign[:].rearrange("p (a t) -> p a t", a=1).to_broadcast([P, N - EARLY, PACK]),
            ALU.mult,
        )
        gather_tokens(TOK, 2 * TOK)
        weigh_chunk(1, score_chunk(1))
        w_codes.append(keep.tile([P, HALF], U32, name="w_codes1", tag="g_early", align_bytes=64))
        gather_tokens(2 * TOK, S)
        weigh_chunk(2, score_chunk(2))
        last_tiles = score_chunk(3)

        out_view = out.rearrange("(j p) v -> p j v", p=P)
        z_grouped = [keep.tile([P, PAS, PACK], BF16, name="z_grouped%d" % c, align_bytes=64) for c in range(CHUNKS)]
        def pool(c):
            nc.vector.tensor_tensor(
                z_grouped[c][:].rearrange("p (c i) t -> p c t i", i=4),
                planes[c][:, :, 0, :].rearrange("p t (c i) -> p c t i", i=4),
                planes[c][:, :, 1, :].rearrange("p t (c i) -> p c t i", i=4),
                ALU.max,
            )

        z_codes = [keep.tile([P, PAS], U32, name="z_codes%d" % c, align_bytes=64) for c in range(CHUNKS)]
        z_scales = [keep.tile([P, PAS], U8, name="z_scales%d" % c, align_bytes=64) for c in range(CHUNKS)]

        def quantize(c):
            nc.vector.quantize_mx(out=z_codes[c][:].bitcast(FP8X4), scales=z_scales[c][:], in_=z_grouped[c][:].rearrange("p v t -> p (v t)"))

        def values(c, j0, count, slot, on_vector):
            acc = bank(slot)
            for j in range(count):
                m0 = (j0 + j) * P % HALF
                nc.tensor.matmul_mx(
                    out=acc[:, j * PAS : (j + 1) * PAS],
                    lhsT=w_codes[j0 // 2][:, m0 : m0 + P].bitcast(FP8X4),
                    lhsT_scale=w_scales[j0 // 2][:, m0 : m0 + P],
                    rhs=z_codes[c][:].bitcast(FP8X4),
                    rhs_scale=z_scales[c][:],
                    start=True,
                    stop=True,
                )
            res = keep.tile([P, count, PAS], F32, name="res%d_%d" % (c, j0), align_bytes=LINE)
            sums = acc[:, 0 : count * PAS].rearrange("p (j v) -> p j v", j=count)
            place = out_view[:, j0 : j0 + count, c * PAS : (c + 1) * PAS]
            if on_vector:
                nc.vector.tensor_copy(res[:], sums)
            else:
                nc.scalar.copy(res[:], sums)
            nc.sync.dma_start(out=place, in_=res[:])

        pool(0)
        quantize_w(1)
        quantize(0)
        pool(1)
        values(0, 0, 2, 7, True)
        values(0, 2, 2, 0, False)
        weigh_chunk(3, last_tiles)
        quantize(1)
        pool(2)
        quantize(2)
        pool(3)
        quantize(3)
        values(1, 0, 2, 1, False)
        values(1, 2, 2, 2, False)
        values(2, 0, 2, 3, False)
        values(2, 2, 2, 7, False)
        for j, slot in enumerate((5, 6, 0, 4)):
            values(3, j, 1, slot, j % 2 == 1)
